import numpy as np
import ml_dtypes


def mxq(x, axis, fmt="e4m3"):
    dtype, down = {"e4m3": (ml_dtypes.float8_e4m3fn, 7), "e5m2": (ml_dtypes.float8_e5m2, 14)}[fmt]
    v = np.moveaxis(np.asarray(x, np.float32).astype(ml_dtypes.bfloat16).astype(np.float64), axis, -1)
    blocks = v.reshape(v.shape[:-1] + (-1, 32))
    amax = np.abs(blocks).max(-1, keepdims=True)
    byte = np.maximum(np.where(amax > 0, np.frexp(amax)[1] - 1 + 127, 0) - down, 1)
    scale = np.exp2(byte - 127.0)
    codes = (blocks / scale).astype(np.float32).astype(dtype).astype(np.float64)
    return np.moveaxis((codes * scale).reshape(v.shape), -1, axis)


WIDE = False


def mx_kscale(k):
    if not WIDE:
        return np.ones(k)
    levels = np.array([10, -10, 5, -5, 0])
    if k % 512:
        return np.exp2(np.random.permutation(np.resize(levels, k // 32))).repeat(32)
    a = np.empty((k // 512, 16))
    for p in range(k // 512):
        a[p, :8] = np.random.permutation(np.resize(levels, 8))
        for g in range(8):
            far = levels[np.abs(levels - a[p, g]) >= 10]
            a[p, g + 8] = far[np.random.randint(len(far))]
    return np.exp2(a.ravel()).repeat(32)


def f64(x):
    return np.asarray(x).astype(np.float64)


def striped(idx):
    return np.tile(idx.reshape(-1, 16).T, (8, 1)).astype(np.uint16)


def unstriped(offs):
    return offs[:16].T.reshape(-1).astype(np.int64)


def pack_weight(w):
    k, n = w.shape
    w = f64(np.asarray(w, np.float32).astype(ml_dtypes.bfloat16)).reshape(k // 32, 32, n)
    amax = np.abs(w).max(1)
    byte = np.clip(np.where(amax > 0, np.frexp(amax)[1] - 1 + 127 - 7, 1), 1, 254)
    scaled = (w * np.exp2(127.0 - byte)[:, None, :]).reshape(k, n).astype(np.float32)
    words = np.ascontiguousarray(scaled.reshape(k // 512, 128, 4, n).transpose(0, 1, 3, 2)).astype(ml_dtypes.float8_e4m3fn).view(np.uint8)
    return words, np.ascontiguousarray(byte.astype(np.uint8).reshape(k // 512, 16, n))


def unpack_weight(words, scales):
    g, p, n, _ = words.shape
    vals = np.ascontiguousarray(words).view(ml_dtypes.float8_e4m3fn).astype(np.float64) * np.repeat(np.exp2(scales.astype(np.float64) - 127.0), 8, axis=1)[..., None]
    return vals.transpose(0, 1, 3, 2).reshape(g * 512, n)


def gelu(v):
    return 0.5 * v * (1.0 + np.tanh(np.sqrt(2.0 / np.pi) * (v + 0.044715 * v**3)))


K, T, S, N = 512, 512, 1024, 2048


def setup_inputs():
    n = np.random.standard_normal
    s = mx_kscale(K)[:, None]
    packed = pack_weight(n((K, N)) / np.sqrt(K) / s)
    return {
        "w_words": packed[0],
        "w_scales": packed[1],
        "xT": (n((K, T)) * s).astype(np.float32),
        "b": (0.3 * n((S, 1))).astype(np.float32),
        "offs": striped(np.sort(np.random.permutation(N)[:S])),
    }


def reference(w_words, w_scales, xT, b, offs):
    idx = unstriped(offs)
    wq = unpack_weight(w_words, w_scales)[:, idx]
    return gelu((wq.T @ mxq(f64(xT), 0, "e4m3")) + f64(b))

@@ -1,0 +1,89 @@
+from contextlib import ExitStack
+
+import concourse.mybir as mybir
+from concourse.masks import make_identity
+
+K, T, S, N = 512, 512, 1024, 2048
+FLOPS = 2 * K * T * S
+F32 = mybir.dt.float32
+BF16 = mybir.dt.bfloat16
+I32 = mybir.dt.int32
+U32 = mybir.dt.uint32
+U16 = mybir.dt.uint16
+U8 = mybir.dt.uint8
+FP8X4 = mybir.dt.float8_e4m3fn_x4
+GELU = mybir.ActivationFunctionType.Gelu_apprx_tanh
+P = 128
+HALF = T // 2
+WORD_CUTS = (0, 160, 384, 640, 1024)
+LOAD_CUTS = (0, 1184, 1408, 2048)
+SCALAR_COLS = (256, 256)
+
+
+def tile_picked_neuron_lin_gelu_srt_p_kernel(tc, w_words, w_scales, xT, b, offs, out):
+    nc = tc.nc
+    with ExitStack() as ctx:
+        keep = ctx.enter_context(tc.tile_pool(name="keep", bufs=1))
+        res = ctx.enter_context(tc.tile_pool(name="res", bufs=8))
+        psum_b = ctx.enter_context(tc.psum_pool(name="psum_b", bufs=1))
+        psum = ctx.enter_context(tc.psum_pool(name="psum", bufs=7))
+
+        scale_table = keep.tile([P, N], U8, name="scale_table", align_bytes=64)
+        nc.gpsimd.memset(scale_table[:].bitcast(I32), 0)
+        bias_rows = keep.tile([P, P], F32, name="bias_rows")
+        nc.vector.memset(bias_rows[:], 0.0)
+
+        warm = keep.tile([P, 1], F32, name="warm")
+        zero = keep.tile([P, 1], F32, name="zero")
+        nc.vector.memset(zero[:], 0.0)
+        nc.scalar.activation(warm[:], zero[:], GELU)
+        offsets = keep.tile([P, S // 16], U16, name="offsets")
+        nc.sync.dma_start(offsets[:], offs)
+        x_rows = xT.rearrange("(p j) t -> p j t", j=4)
+        raws = [keep.tile([P, 4, HALF], F32, name="raw%d" % h) for h in range(2)]
+        nc.sync.dma_start(raws[0][:], x_rows[:, :, 0:HALF])
+        for q in range(4):
+            nc.sync.dma_start(scale_table[32 * q : 32 * q + 4, :].bitcast(I32), w_scales[0, 4 * q : 4 * q + 4, :].bitcast(I32))
+        nc.sync.dma_start(bias_rows[0 : S // P, :], b.rearrange("(c p) o -> c (p o)", p=P))
+        nc.sync.dma_start(raws[1][:], x_rows[:, :, HALF:T])
+
+        word_table = keep.tile([P, N], U32, name="word_table", align_bytes=64)
+        w_flat = w_words[0].rearrange("p n r -> p (n r)")
+        for a, z in zip(LOAD_CUTS[:-1], LOAD_CUTS[1:]):
+            nc.sync.dma_start(word_table[:, a:z].bitcast(I32), w_flat[:, 4 * a : 4 * z].bitcast(I32))
+
+        ident = keep.tile([P, P], F32, name="ident")
+        make_identity(nc, ident[:])
+
+        w_scale = keep.tile([P, S], U8, name="w_scale", align_bytes=64)
+        nc.vector.tensor_copy(w_scale[:], scale_table[:].indirect(offsets[:]))
+
+        x_codes = keep.tile([P, T], U32, name="x_codes", align_bytes=64)
+        x_scale = keep.tile([P, T], U8, name="x_scale", align_bytes=64)
+        grouped = keep.tile([P, T, 4], BF16, name="grouped", align_bytes=64)
+        for h in range(2):
+            dst = grouped[:, h * HALF : (h + 1) * HALF, :].rearrange("p (c i) j -> p c j i", i=4)
+            src = raws[h][:].rearrange("p j (c i) -> p c j i", i=4)
+            cut = SCALAR_COLS[h] // 4
+            nc.scalar.copy(dst[:, 0:cut], src[:, 0:cut])
+            if cut < HALF // 4:
+                nc.vector.tensor_copy(dst[:, cut:], src[:, cut:])
+        nc.vector.quantize_mx(out=x_codes[:].bitcast(FP8X4), scales=x_scale[:], in_=grouped[:].rearrange("p t j -> p (t j)"))
+
+        bias_ps = psum_b.tile([P, P], F32, name="bias_ps")
+        nc.tensor.transpose(bias_ps[:], bias_rows[:], ident[:])
+        bias = keep.tile([P, S // P], F32, name="bias")
+        nc.scalar.copy(bias[:], bias_ps[:, 0 : S // P])
+        w_codes = keep.tile([P, S], U32, name="w_codes", align_bytes=64)
+        done = 0
+        for a, z in zip(WORD_CUTS[:-1], WORD_CUTS[1:]):
+            nc.vector.tensor_copy(w_codes[:, a:z], word_table[:, 0 : z + N - S].indirect(offsets[:, a // 16 : z // 16]))
+            while (done + 1) * P <= z:
+                rows = slice(done * P, (done + 1) * P)
+                acc = psum.tile([P, T], F32, name="acc")
+                nc.tensor.matmul_mx(out=acc[:], lhsT=w_codes[:, rows].bitcast(FP8X4), lhsT_scale=w_scale[:, rows],
+                                    rhs=x_codes[:].bitcast(FP8X4), rhs_scale=x_scale[:], start=True, stop=True)
+                y = res.tile([P, T], F32, name="y")
+                nc.scalar.activation(y[:], acc[:], GELU, bias=bias[:, done : done + 1])
+                nc.sync.dma_start(out[rows, :], y[:])
+                done = done + 1

@@ -16,15 +16,16 @@ GELU = mybir.ActivationFunctionType.Gelu_apprx_tanh
 P = 128
 HALF = T // 2
 WORD_CUTS = (0, 160, 384, 640, 1024)
-LOAD_CUTS = (0, 1184, 1408, 2048)
-SCALAR_COLS = (256, 256)
+LOAD_CUTS = (0, 1184, 1664, 2048)
+EARLY = 512
+SCALAR_COLS = (256, 96)
 
 
 def tile_picked_neuron_lin_gelu_srt_p_kernel(tc, w_words, w_scales, xT, b, offs, out):
     nc = tc.nc
     with ExitStack() as ctx:
         keep = ctx.enter_context(tc.tile_pool(name="keep", bufs=1))
-        res = ctx.enter_context(tc.tile_pool(name="res", bufs=8))
+        res = ctx.enter_context(tc.tile_pool(name="res", bufs=10))
         psum_b = ctx.enter_context(tc.psum_pool(name="psum_b", bufs=1))
         psum = ctx.enter_context(tc.psum_pool(name="psum", bufs=7))
 
@@ -42,21 +43,27 @@ def tile_picked_neuron_lin_gelu_srt_p_kernel(tc, w_words, w_scales, xT, b, offs,
         x_rows = xT.rearrange("(p j) t -> p j t", j=4)
         raws = [keep.tile([P, 4, HALF], F32, name="raw%d" % h) for h in range(2)]
         nc.sync.dma_start(raws[0][:], x_rows[:, :, 0:HALF])
-        for q in range(4):
-            nc.sync.dma_start(scale_table[32 * q : 32 * q + 4, :].bitcast(I32), w_scales[0, 4 * q : 4 * q + 4, :].bitcast(I32))
+
+        def load_scales(a, z):
+            for q in range(4):
+                nc.sync.dma_start(scale_table[32 * q : 32 * q + 4, a:z].bitcast(I32), w_scales[0, 4 * q : 4 * q + 4, a:z].bitcast(I32))
+
+        load_scales(0, EARLY + N - S)
         nc.sync.dma_start(bias_rows[0 : S // P, :], b.rearrange("(c p) o -> c (p o)", p=P))
         nc.sync.dma_start(raws[1][:], x_rows[:, :, HALF:T])
 
         word_table = keep.tile([P, N], U32, name="word_table", align_bytes=64)
         w_flat = w_words[0].rearrange("p n r -> p (n r)")
         for a, z in zip(LOAD_CUTS[:-1], LOAD_CUTS[1:]):
+            if z == N:
+                load_scales(EARLY + N - S, N)
             nc.sync.dma_start(word_table[:, a:z].bitcast(I32), w_flat[:, 4 * a : 4 * z].bitcast(I32))
 
         ident = keep.tile([P, P], F32, name="ident")
         make_identity(nc, ident[:])
 
-        w_scale = keep.tile([P, S], U8, name="w_scale", align_bytes=64)
-        nc.vector.tensor_copy(w_scale[:], scale_table[:].indirect(offsets[:]))
+        early = keep.tile([P, S // 2], U8, name="early", align_bytes=64)
+        nc.vector.tensor_copy(early[:], scale_table[:, 0 : EARLY + N - S].indirect(offsets[:, 0:32]))
 
         x_codes = keep.tile([P, T], U32, name="x_codes", align_bytes=64)
         x_scale = keep.tile([P, T], U8, name="x_scale", align_bytes=64)
@@ -75,15 +82,35 @@ def tile_picked_neuron_lin_gelu_srt_p_kernel(tc, w_words, w_scales, xT, b, offs,
         bias = keep.tile([P, S // P], F32, name="bias")
         nc.scalar.copy(bias[:], bias_ps[:, 0 : S // P])
         w_codes = keep.tile([P, S], U32, name="w_codes", align_bytes=64)
-        done = 0
-        for a, z in zip(WORD_CUTS[:-1], WORD_CUTS[1:]):
+        late = keep.tile([P, S // 2], U8, name="late", align_bytes=64)
+
+        def gather_words(piece):
+            a, z = WORD_CUTS[piece], WORD_CUTS[piece + 1]
             nc.vector.tensor_copy(w_codes[:, a:z], word_table[:, 0 : z + N - S].indirect(offsets[:, a // 16 : z // 16]))
-            while (done + 1) * P <= z:
-                rows = slice(done * P, (done + 1) * P)
-                acc = psum.tile([P, T], F32, name="acc")
-                nc.tensor.matmul_mx(out=acc[:], lhsT=w_codes[:, rows].bitcast(FP8X4), lhsT_scale=w_scale[:, rows],
-                                    rhs=x_codes[:].bitcast(FP8X4), rhs_scale=x_scale[:], start=True, stop=True)
-                y = res.tile([P, T], F32, name="y")
-                nc.scalar.activation(y[:], acc[:], GELU, bias=bias[:, done : done + 1])
-                nc.sync.dma_start(out[rows, :], y[:])
-                done = done + 1
+
+        def product(t):
+            rows = slice(t * P, (t + 1) * P)
+            plane = early[:, rows] if t < 4 else late[:, (t - 4) * P : (t - 3) * P]
+            parts = 2 if t in (0, S // P - 1) else 1
+            for part in range(parts):
+                cols = slice(part * T // parts, (part + 1) * T // parts)
+                acc = psum.tile([P, T // parts], F32, name="acc")
+                nc.tensor.matmul_mx(out=acc[:], lhsT=w_codes[:, rows].bitcast(FP8X4), lhsT_scale=plane,
+                                    rhs=x_codes[:, cols].bitcast(FP8X4), rhs_scale=x_scale[:, cols], start=True, stop=True)
+                y = res.tile([P, T // parts], F32, name="y")
+                nc.scalar.activation(y[:], acc[:], GELU, bias=bias[:, t : t + 1])
+                nc.sync.dma_start(out[rows, cols], y[:])
+
+        gather_words(0)
+        product(0)
+        gather_words(1)
+        product(1)
+        product(2)
+        gather_words(2)
+        product(3)
+        nc.vector.tensor_copy(late[:], scale_table[:].indirect(offsets[:, 32:64]))
+        product(4)
+        gather_words(3)
+        product(5)
+        product(6)
+        product(7)

@@ -17,21 +17,23 @@ P = 128
 HALF = T // 2
 WORD_CUTS = (0, 160, 384, 640, 1024)
 LOAD_CUTS = (0, 1184, 1664, 2048)
-EARLY = 512
-SCALAR_COLS = (256, 96)
+EARLY = 384
+SCALAR_COLS = (256, 80)
 
 
 def tile_picked_neuron_lin_gelu_srt_p_kernel(tc, w_words, w_scales, xT, b, offs, out):
     nc = tc.nc
     with ExitStack() as ctx:
         keep = ctx.enter_context(tc.tile_pool(name="keep", bufs=1))
+        reuse = ctx.enter_context(tc.tile_pool(name="reuse", bufs=1))
         res = ctx.enter_context(tc.tile_pool(name="res", bufs=10))
         psum_b = ctx.enter_context(tc.psum_pool(name="psum_b", bufs=1))
         psum = ctx.enter_context(tc.psum_pool(name="psum", bufs=7))
 
         scale_table = keep.tile([P, N], U8, name="scale_table", align_bytes=64)
-        nc.gpsimd.memset(scale_table[:].bitcast(I32), 0)
-        bias_rows = keep.tile([P, P], F32, name="bias_rows")
+        nc.gpsimd.memset(scale_table[:, 0 : EARLY + N - S].bitcast(I32), 0)
+        nc.gpsimd.memset(scale_table[:, EARLY + N - S : N].bitcast(I32), 0)
+        bias_rows = reuse.tile([P, P], F32, name="bias_rows", align_bytes=64, offset=0)
         nc.vector.memset(bias_rows[:], 0.0)
 
         warm = keep.tile([P, 1], F32, name="warm")
@@ -49,8 +51,8 @@ def tile_picked_neuron_lin_gelu_srt_p_kernel(tc, w_words, w_scales, xT, b, offs,
                 nc.sync.dma_start(scale_table[32 * q : 32 * q + 4, a:z].bitcast(I32), w_scales[0, 4 * q : 4 * q + 4, a:z].bitcast(I32))
 
         load_scales(0, EARLY + N - S)
-        nc.sync.dma_start(bias_rows[0 : S // P, :], b.rearrange("(c p) o -> c (p o)", p=P))
         nc.sync.dma_start(raws[1][:], x_rows[:, :, HALF:T])
+        nc.sync.dma_start(bias_rows[0 : S // P, :], b.rearrange("(c p) o -> c (p o)", p=P))
 
         word_table = keep.tile([P, N], U32, name="word_table", align_bytes=64)
         w_flat = w_words[0].rearrange("p n r -> p (n r)")
@@ -62,8 +64,8 @@ def tile_picked_neuron_lin_gelu_srt_p_kernel(tc, w_words, w_scales, xT, b, offs,
         ident = keep.tile([P, P], F32, name="ident")
         make_identity(nc, ident[:])
 
-        early = keep.tile([P, S // 2], U8, name="early", align_bytes=64)
-        nc.vector.tensor_copy(early[:], scale_table[:, 0 : EARLY + N - S].indirect(offsets[:, 0:32]))
+        early = keep.tile([P, EARLY], U8, name="early", align_bytes=64)
+        nc.vector.tensor_copy(early[:], scale_table[:, 0 : EARLY + N - S].indirect(offsets[:, 0 : EARLY // 16]))
 
         x_codes = keep.tile([P, T], U32, name="x_codes", align_bytes=64)
         x_scale = keep.tile([P, T], U8, name="x_scale", align_bytes=64)
@@ -81,8 +83,8 @@ def tile_picked_neuron_lin_gelu_srt_p_kernel(tc, w_words, w_scales, xT, b, offs,
         nc.tensor.transpose(bias_ps[:], bias_rows[:], ident[:])
         bias = keep.tile([P, S // P], F32, name="bias")
         nc.scalar.copy(bias[:], bias_ps[:, 0 : S // P])
-        w_codes = keep.tile([P, S], U32, name="w_codes", align_bytes=64)
-        late = keep.tile([P, S // 2], U8, name="late", align_bytes=64)
+        w_codes = reuse.tile([P, S], U32, name="w_codes", align_bytes=64, offset=0)
+        late = keep.tile([P, S - EARLY], U8, name="late", align_bytes=64)
 
         def gather_words(piece):
             a, z = WORD_CUTS[piece], WORD_CUTS[piece + 1]
@@ -90,7 +92,7 @@ def tile_picked_neuron_lin_gelu_srt_p_kernel(tc, w_words, w_scales, xT, b, offs,
 
         def product(t):
             rows = slice(t * P, (t + 1) * P)
-            plane = early[:, rows] if t < 4 else late[:, (t - 4) * P : (t - 3) * P]
+            plane = early[:, rows] if t < 3 else late[:, (t - 3) * P : (t - 2) * P]
             parts = 2 if t in (0, S // P - 1) else 1
             for part in range(parts):
                 cols = slice(part * T // parts, (part + 1) * T // parts)
@@ -107,9 +109,10 @@ def tile_picked_neuron_lin_gelu_srt_p_kernel(tc, w_words, w_scales, xT, b, offs,
         product(1)
         product(2)
         gather_words(2)
+        nc.vector.tensor_copy(late[:, 0:256], scale_table[:].indirect(offsets[:, 24:40]))
         product(3)
-        nc.vector.tensor_copy(late[:], scale_table[:].indirect(offsets[:, 32:64]))
         product(4)
+        nc.vector.tensor_copy(late[:, 256:640], scale_table[:].indirect(offsets[:, 40:64]))
         gather_words(3)
         product(5)
         product(6)

@@ -18,7 +18,7 @@ HALF = T // 2
 WORD_CUTS = (0, 160, 384, 640, 1024)
 LOAD_CUTS = (0, 1184, 1664, 2048)
 EARLY = 384
-SCALAR_COLS = (256, 80)
+SCALAR_COLS = (384, 160)
 
 
 def tile_picked_neuron_lin_gelu_srt_p_kernel(tc, w_words, w_scales, xT, b, offs, out):
@@ -43,15 +43,15 @@ def tile_picked_neuron_lin_gelu_srt_p_kernel(tc, w_words, w_scales, xT, b, offs,
         offsets = keep.tile([P, S // 16], U16, name="offsets")
         nc.sync.dma_start(offsets[:], offs)
         x_rows = xT.rearrange("(p j) t -> p j t", j=4)
-        raws = [keep.tile([P, 4, HALF], F32, name="raw%d" % h) for h in range(2)]
-        nc.sync.dma_start(raws[0][:], x_rows[:, :, 0:HALF])
+        raws = [keep.tile([P, 2, T], F32, name="raw%d" % h) for h in range(2)]
+        nc.sync.dma_start(raws[0][:], x_rows[:, 0:2, :])
 
         def load_scales(a, z):
             for q in range(4):
                 nc.sync.dma_start(scale_table[32 * q : 32 * q + 4, a:z].bitcast(I32), w_scales[0, 4 * q : 4 * q + 4, a:z].bitcast(I32))
 
         load_scales(0, EARLY + N - S)
-        nc.sync.dma_start(raws[1][:], x_rows[:, :, HALF:T])
+        nc.sync.dma_start(raws[1][:], x_rows[:, 2:4, :])
         nc.sync.dma_start(bias_rows[0 : S // P, :], b.rearrange("(c p) o -> c (p o)", p=P))
 
         word_table = keep.tile([P, N], U32, name="word_table", align_bytes=64)
@@ -71,12 +71,11 @@ def tile_picked_neuron_lin_gelu_srt_p_kernel(tc, w_words, w_scales, xT, b, offs,
         x_scale = keep.tile([P, T], U8, name="x_scale", align_bytes=64)
         grouped = keep.tile([P, T, 4], BF16, name="grouped", align_bytes=64)
         for h in range(2):
-            dst = grouped[:, h * HALF : (h + 1) * HALF, :].rearrange("p (c i) j -> p c j i", i=4)
-            src = raws[h][:].rearrange("p j (c i) -> p c j i", i=4)
-            cut = SCALAR_COLS[h] // 4
+            dst = grouped[:, :, 2 * h : 2 * h + 2]
+            src = raws[h][:].rearrange("p j t -> p t j")
+            cut = SCALAR_COLS[h]
             nc.scalar.copy(dst[:, 0:cut], src[:, 0:cut])
-            if cut < HALF // 4:
-                nc.vector.tensor_copy(dst[:, cut:], src[:, cut:])
+            nc.vector.tensor_copy(dst[:, cut:], src[:, cut:])
         nc.vector.quantize_mx(out=x_codes[:].bitcast(FP8X4), scales=x_scale[:], in_=grouped[:].rearrange("p t j -> p (t j)"))
 
         bias_ps = psum_b.tile([P, P], F32, name="bias_ps")

@@ -14,11 +14,10 @@ U8 = mybir.dt.uint8
 FP8X4 = mybir.dt.float8_e4m3fn_x4
 GELU = mybir.ActivationFunctionType.Gelu_apprx_tanh
 P = 128
+SPARE = N - S
 HALF = T // 2
-WORD_CUTS = (0, 160, 384, 640, 1024)
-LOAD_CUTS = (0, 1184, 1664, 2048)
-EARLY = 384
-SCALAR_COLS = (384, 160)
+LOAD_CUTS = (0, 1184, 1792, 2048)
+EARLY = 512
 
 
 def tile_picked_neuron_lin_gelu_srt_p_kernel(tc, w_words, w_scales, xT, b, offs, out):
@@ -31,8 +30,8 @@ def tile_picked_neuron_lin_gelu_srt_p_kernel(tc, w_words, w_scales, xT, b, offs,
         psum = ctx.enter_context(tc.psum_pool(name="psum", bufs=7))
 
         scale_table = keep.tile([P, N], U8, name="scale_table", align_bytes=64)
-        nc.gpsimd.memset(scale_table[:, 0 : EARLY + N - S].bitcast(I32), 0)
-        nc.gpsimd.memset(scale_table[:, EARLY + N - S : N].bitcast(I32), 0)
+        nc.gpsimd.memset(scale_table[:, 0 : EARLY + SPARE].bitcast(I32), 0)
+        nc.gpsimd.memset(scale_table[:, EARLY + SPARE : N].bitcast(I32), 0)
         bias_rows = reuse.tile([P, P], F32, name="bias_rows", align_bytes=64, offset=0)
         nc.vector.memset(bias_rows[:], 0.0)
 
@@ -41,16 +40,16 @@ def tile_picked_neuron_lin_gelu_srt_p_kernel(tc, w_words, w_scales, xT, b, offs,
         nc.vector.memset(zero[:], 0.0)
         nc.scalar.activation(warm[:], zero[:], GELU)
         offsets = keep.tile([P, S // 16], U16, name="offsets")
-        nc.sync.dma_start(offsets[:], offs)
         x_rows = xT.rearrange("(p j) t -> p j t", j=4)
         raws = [keep.tile([P, 2, T], F32, name="raw%d" % h) for h in range(2)]
+        nc.sync.dma_start(offsets[:], offs)
         nc.sync.dma_start(raws[0][:], x_rows[:, 0:2, :])
 
         def load_scales(a, z):
-            for q in range(4):
+            for q in (0, 2, 1, 3):
                 nc.sync.dma_start(scale_table[32 * q : 32 * q + 4, a:z].bitcast(I32), w_scales[0, 4 * q : 4 * q + 4, a:z].bitcast(I32))
 
-        load_scales(0, EARLY + N - S)
+        load_scales(0, EARLY + SPARE)
         nc.sync.dma_start(raws[1][:], x_rows[:, 2:4, :])
         nc.sync.dma_start(bias_rows[0 : S // P, :], b.rearrange("(c p) o -> c (p o)", p=P))
 
@@ -58,61 +57,75 @@ def tile_picked_neuron_lin_gelu_srt_p_kernel(tc, w_words, w_scales, xT, b, offs,
         w_flat = w_words[0].rearrange("p n r -> p (n r)")
         for a, z in zip(LOAD_CUTS[:-1], LOAD_CUTS[1:]):
             if z == N:
-                load_scales(EARLY + N - S, N)
+                load_scales(EARLY + SPARE, N)
             nc.sync.dma_start(word_table[:, a:z].bitcast(I32), w_flat[:, 4 * a : 4 * z].bitcast(I32))
 
         ident = keep.tile([P, P], F32, name="ident")
         make_identity(nc, ident[:])
 
+        def gather(dst, table, a, z):
+            nc.vector.tensor_copy(dst, table[:, 0 : z + SPARE].indirect(offsets[:, a // 16 : z // 16]))
+
         early = keep.tile([P, EARLY], U8, name="early", align_bytes=64)
-        nc.vector.tensor_copy(early[:], scale_table[:, 0 : EARLY + N - S].indirect(offsets[:, 0 : EARLY // 16]))
+        gather(early[:], scale_table, 0, EARLY)
 
         x_codes = keep.tile([P, T], U32, name="x_codes", align_bytes=64)
         x_scale = keep.tile([P, T], U8, name="x_scale", align_bytes=64)
-        grouped = keep.tile([P, T, 4], BF16, name="grouped", align_bytes=64)
-        for h in range(2):
-            dst = grouped[:, :, 2 * h : 2 * h + 2]
-            src = raws[h][:].rearrange("p j t -> p t j")
-            cut = SCALAR_COLS[h]
-            nc.scalar.copy(dst[:, 0:cut], src[:, 0:cut])
-            nc.vector.tensor_copy(dst[:, cut:], src[:, cut:])
-        nc.vector.quantize_mx(out=x_codes[:].bitcast(FP8X4), scales=x_scale[:], in_=grouped[:].rearrange("p t j -> p (t j)"))
+        grouped = [keep.tile([P, HALF, 4], BF16, name="grouped%d" % u, align_bytes=64) for u in range(2)]
+
+        def cast(copy, h, a, z):
+            u = a // HALF
+            copy(grouped[u][:, a - u * HALF : z - u * HALF, 2 * h : 2 * h + 2], raws[h][:, :, a:z].rearrange("p j t -> p t j"))
+
+        cast(nc.scalar.copy, 0, 0, HALF)
+        cast(nc.scalar.copy, 0, HALF, 384)
+        cast(nc.vector.tensor_copy, 0, 384, T)
+        cast(nc.vector.tensor_copy, 1, 0, 160)
+        cast(nc.scalar.copy, 1, 160, HALF)
+        cast(nc.scalar.copy, 1, HALF, 416)
+        cast(nc.vector.tensor_copy, 1, 416, T)
+        for u in range(2):
+            cols = slice(u * HALF, (u + 1) * HALF)
+            nc.vector.quantize_mx(out=x_codes[:, cols].bitcast(FP8X4), scales=x_scale[:, cols], in_=grouped[u][:].rearrange("p t j -> p (t j)"))
 
         bias_ps = psum_b.tile([P, P], F32, name="bias_ps")
         nc.tensor.transpose(bias_ps[:], bias_rows[:], ident[:])
         bias = keep.tile([P, S // P], F32, name="bias")
         nc.scalar.copy(bias[:], bias_ps[:, 0 : S // P])
-        w_codes = reuse.tile([P, S], U32, name="w_codes", align_bytes=64, offset=0)
-        late = keep.tile([P, S - EARLY], U8, name="late", align_bytes=64)
 
-        def gather_words(piece):
-            a, z = WORD_CUTS[piece], WORD_CUTS[piece + 1]
-            nc.vector.tensor_copy(w_codes[:, a:z], word_table[:, 0 : z + N - S].indirect(offsets[:, a // 16 : z // 16]))
-
-        def product(t):
+        def product(t, codes, plane):
             rows = slice(t * P, (t + 1) * P)
-            plane = early[:, rows] if t < 3 else late[:, (t - 3) * P : (t - 2) * P]
-            parts = 2 if t in (0, S // P - 1) else 1
+            parts = 2 if t in (0, 1, S // P - 1) else 1
+            y = res.tile([P, T], F32, name="y")
             for part in range(parts):
                 cols = slice(part * T // parts, (part + 1) * T // parts)
                 acc = psum.tile([P, T // parts], F32, name="acc")
-                nc.tensor.matmul_mx(out=acc[:], lhsT=w_codes[:, rows].bitcast(FP8X4), lhsT_scale=plane,
+                nc.tensor.matmul_mx(out=acc[:], lhsT=codes.bitcast(FP8X4), lhsT_scale=plane,
                                     rhs=x_codes[:, cols].bitcast(FP8X4), rhs_scale=x_scale[:, cols], start=True, stop=True)
-                y = res.tile([P, T // parts], F32, name="y")
-                nc.scalar.activation(y[:], acc[:], GELU, bias=bias[:, t : t + 1])
-                nc.sync.dma_start(out[rows, cols], y[:])
+                nc.scalar.activation(y[:, cols], acc[:], GELU, bias=bias[:, t : t + 1])
+                if t in (0, S // P - 1):
+                    nc.sync.dma_start(out[rows, cols], y[:, cols])
+            if t not in (0, S // P - 1):
+                nc.sync.dma_start(out[rows, :], y[:])
 
-        gather_words(0)
-        product(0)
-        gather_words(1)
-        product(1)
-        product(2)
-        gather_words(2)
-        nc.vector.tensor_copy(late[:, 0:256], scale_table[:].indirect(offsets[:, 24:40]))
-        product(3)
-        product(4)
-        nc.vector.tensor_copy(late[:, 256:640], scale_table[:].indirect(offsets[:, 40:64]))
-        gather_words(3)
-        product(5)
-        product(6)
-        product(7)
+        w_codes = reuse.tile([P, S], U32, name="w_codes", align_bytes=64, offset=0)
+        late = keep.tile([P, S - EARLY], U8, name="late", align_bytes=64)
+
+        def tile_product(t):
+            c = t * P
+            product(t, w_codes[:, c : c + P], early[:, c : c + P] if c < EARLY else late[:, c - EARLY : c - EARLY + P])
+
+        gather(w_codes[:, 0:160], word_table, 0, 160)
+        tile_product(0)
+        gather(w_codes[:, 160:384], word_table, 160, 384)
+        tile_product(1)
+        tile_product(2)
+        gather(w_codes[:, 384:768], word_table, 384, 768)
+        tile_product(3)
+        gather(late[:, 0:256], scale_table, 512, 768)
+        tile_product(4)
+        tile_product(5)
+        gather(late[:, 256:512], scale_table, 768, S)
+        gather(w_codes[:, 768:S], word_table, 768, S)
+        tile_product(6)
+        tile_product(7)

@@ -31,25 +31,25 @@ def tile_picked_neuron_lin_gelu_srt_p_kernel(tc, w_words, w_scales, xT, b, offs,
 
         scale_table = keep.tile([P, N], U8, name="scale_table", align_bytes=64)
         nc.gpsimd.memset(scale_table[:, 0 : EARLY + SPARE].bitcast(I32), 0)
+        zero = keep.tile([P, 1], F32, name="zero")
+        nc.gpsimd.memset(zero[:], 0.0)
         nc.gpsimd.memset(scale_table[:, EARLY + SPARE : N].bitcast(I32), 0)
         bias_rows = reuse.tile([P, P], F32, name="bias_rows", align_bytes=64, offset=0)
         nc.vector.memset(bias_rows[:], 0.0)
 
-        warm = keep.tile([P, 1], F32, name="warm")
-        zero = keep.tile([P, 1], F32, name="zero")
-        nc.vector.memset(zero[:], 0.0)
-        nc.scalar.activation(warm[:], zero[:], GELU)
         offsets = keep.tile([P, S // 16], U16, name="offsets")
         x_rows = xT.rearrange("(p j) t -> p j t", j=4)
         raws = [keep.tile([P, 2, T], F32, name="raw%d" % h) for h in range(2)]
         nc.sync.dma_start(offsets[:], offs)
         nc.sync.dma_start(raws[0][:], x_rows[:, 0:2, :])
 
-        def load_scales(a, z):
-            for q in (0, 2, 1, 3):
-                nc.sync.dma_start(scale_table[32 * q : 32 * q + 4, a:z].bitcast(I32), w_scales[0, 4 * q : 4 * q + 4, a:z].bitcast(I32))
+        def load_scales(a, z, queues):
+            for q in (0, 3, 2, 1):
+                queues[q % 2].dma_start(scale_table[32 * q : 32 * q + 4, a:z].bitcast(I32), w_scales[0, 4 * q : 4 * q + 4, a:z].bitcast(I32))
 
-        load_scales(0, EARLY + SPARE)
+        load_scales(0, EARLY + SPARE, (nc.sync, nc.scalar))
+        warm = keep.tile([P, 1], F32, name="warm")
+        nc.scalar.activation(warm[:], zero[:], GELU)
         nc.sync.dma_start(raws[1][:], x_rows[:, 2:4, :])
         nc.sync.dma_start(bias_rows[0 : S // P, :], b.rearrange("(c p) o -> c (p o)", p=P))
 
@@ -57,7 +57,7 @@ def tile_picked_neuron_lin_gelu_srt_p_kernel(tc, w_words, w_scales, xT, b, offs,
         w_flat = w_words[0].rearrange("p n r -> p (n r)")
         for a, z in zip(LOAD_CUTS[:-1], LOAD_CUTS[1:]):
             if z == N:
-                load_scales(EARLY + SPARE, N)
+                load_scales(EARLY + SPARE, N, (nc.sync, nc.sync))
             nc.sync.dma_start(word_table[:, a:z].bitcast(I32), w_flat[:, 4 * a : 4 * z].bitcast(I32))
 
         ident = keep.tile([P, P], F32, name="ident")
@@ -95,11 +95,11 @@ def tile_picked_neuron_lin_gelu_srt_p_kernel(tc, w_words, w_scales, xT, b, offs,
 
         def product(t, codes, plane):
             rows = slice(t * P, (t + 1) * P)
-            parts = 2 if t in (0, 1, S // P - 1) else 1
+            cuts = {0: (0, 128, 256, T), 1: (0, HALF, T), S // P - 1: (0, HALF, T)}.get(t, (0, T))
             y = res.tile([P, T], F32, name="y")
-            for part in range(parts):
-                cols = slice(part * T // parts, (part + 1) * T // parts)
-                acc = psum.tile([P, T // parts], F32, name="acc")
+            for a, z in zip(cuts[:-1], cuts[1:]):
+                cols = slice(a, z)
+                acc = psum.tile([P, z - a], F32, name="acc")
                 nc.tensor.matmul_mx(out=acc[:], lhsT=codes.bitcast(FP8X4), lhsT_scale=plane,
                                     rhs=x_codes[:, cols].bitcast(FP8X4), rhs_scale=x_scale[:, cols], start=True, stop=True)
                 nc.scalar.activation(y[:, cols], acc[:], GELU, bias=bias[:, t : t + 1])

@@ -16,7 +16,7 @@ GELU = mybir.ActivationFunctionType.Gelu_apprx_tanh
 P = 128
 SPARE = N - S
 HALF = T // 2
-LOAD_CUTS = (0, 1184, 1792, 2048)
+LOAD_CUTS = (0, 1184, 1408, 1792, 2048)
 EARLY = 512
 
 

@@ -25,7 +25,7 @@ def tile_picked_neuron_lin_gelu_srt_p_kernel(tc, w_words, w_scales, xT, b, offs,
     with ExitStack() as ctx:
         keep = ctx.enter_context(tc.tile_pool(name="keep", bufs=1))
         reuse = ctx.enter_context(tc.tile_pool(name="reuse", bufs=1))
-        res = ctx.enter_context(tc.tile_pool(name="res", bufs=10))
+        res = ctx.enter_context(tc.tile_pool(name="res", bufs=12))
         psum_b = ctx.enter_context(tc.psum_pool(name="psum_b", bufs=1))
         psum = ctx.enter_context(tc.psum_pool(name="psum", bufs=7))
 
@@ -95,18 +95,15 @@ def tile_picked_neuron_lin_gelu_srt_p_kernel(tc, w_words, w_scales, xT, b, offs,
 
         def product(t, codes, plane):
             rows = slice(t * P, (t + 1) * P)
-            cuts = {0: (0, 128, 256, T), 1: (0, HALF, T), S // P - 1: (0, HALF, T)}.get(t, (0, T))
-            y = res.tile([P, T], F32, name="y")
+            cuts = {0: (0, HALF // 2, HALF, T), 1: (0, HALF, T), 2: (0, HALF, T)}.get(t, (0, T))
             for a, z in zip(cuts[:-1], cuts[1:]):
                 cols = slice(a, z)
                 acc = psum.tile([P, z - a], F32, name="acc")
                 nc.tensor.matmul_mx(out=acc[:], lhsT=codes.bitcast(FP8X4), lhsT_scale=plane,
                                     rhs=x_codes[:, cols].bitcast(FP8X4), rhs_scale=x_scale[:, cols], start=True, stop=True)
-                nc.scalar.activation(y[:, cols], acc[:], GELU, bias=bias[:, t : t + 1])
-                if t in (0, S // P - 1):
-                    nc.sync.dma_start(out[rows, cols], y[:, cols])
-            if t not in (0, S // P - 1):
-                nc.sync.dma_start(out[rows, :], y[:])
+                y = res.tile([P, z - a], F32, name="y")
+                nc.scalar.activation(y[:], acc[:], GELU, bias=bias[:, t : t + 1])
+                nc.sync.dma_start(out[rows, cols], y[:])
 
         w_codes = reuse.tile([P, S], U32, name="w_codes", align_bytes=64, offset=0)
         late = keep.tile([P, S - EARLY], U8, name="late", align_bytes=64)

@@ -1,7 +1,6 @@
 from contextlib import ExitStack
 
 import concourse.mybir as mybir
-from concourse.masks import make_identity
 
 K, T, S, N = 512, 512, 1024, 2048
 FLOPS = 2 * K * T * S
@@ -12,12 +11,13 @@ U32 = mybir.dt.uint32
 U16 = mybir.dt.uint16
 U8 = mybir.dt.uint8
 FP8X4 = mybir.dt.float8_e4m3fn_x4
+ALU = mybir.AluOpType
 GELU = mybir.ActivationFunctionType.Gelu_apprx_tanh
 P = 128
 SPARE = N - S
 HALF = T // 2
-LOAD_CUTS = (0, 1184, 1408, 1792, 2048)
-EARLY = 512
+TILES = S // P
+BIAS_ROW = 32 - TILES
 
 
 def tile_picked_neuron_lin_gelu_srt_p_kernel(tc, w_words, w_scales, xT, b, offs, out):
@@ -30,99 +30,109 @@ def tile_picked_neuron_lin_gelu_srt_p_kernel(tc, w_words, w_scales, xT, b, offs,
         psum = ctx.enter_context(tc.psum_pool(name="psum", bufs=7))
 
         scale_table = keep.tile([P, N], U8, name="scale_table", align_bytes=64)
-        nc.gpsimd.memset(scale_table[:, 0 : EARLY + SPARE].bitcast(I32), 0)
+        nc.vector.memset(scale_table[:].bitcast(I32), 0)
         zero = keep.tile([P, 1], F32, name="zero")
-        nc.gpsimd.memset(zero[:], 0.0)
-        nc.gpsimd.memset(scale_table[:, EARLY + SPARE : N].bitcast(I32), 0)
+        nc.vector.memset(zero[:], 0.0)
         bias_rows = reuse.tile([P, P], F32, name="bias_rows", align_bytes=64, offset=0)
-        nc.vector.memset(bias_rows[:], 0.0)
+        for lo, hi in ((0, BIAS_ROW), (32, 64), (64, P)):
+            nc.gpsimd.memset(bias_rows[lo:hi, :], 0.0)
 
         offsets = keep.tile([P, S // 16], U16, name="offsets")
         x_rows = xT.rearrange("(p j) t -> p j t", j=4)
-        raws = [keep.tile([P, 2, T], F32, name="raw%d" % h) for h in range(2)]
-        nc.sync.dma_start(offsets[:], offs)
-        nc.sync.dma_start(raws[0][:], x_rows[:, 0:2, :])
-
-        def load_scales(a, z, queues):
-            for q in (0, 3, 2, 1):
-                queues[q % 2].dma_start(scale_table[32 * q : 32 * q + 4, a:z].bitcast(I32), w_scales[0, 4 * q : 4 * q + 4, a:z].bitcast(I32))
-
-        load_scales(0, EARLY + SPARE, (nc.sync, nc.scalar))
-        warm = keep.tile([P, 1], F32, name="warm")
-        nc.scalar.activation(warm[:], zero[:], GELU)
-        nc.sync.dma_start(raws[1][:], x_rows[:, 2:4, :])
-        nc.sync.dma_start(bias_rows[0 : S // P, :], b.rearrange("(c p) o -> c (p o)", p=P))
-
+        raws = [keep.tile([P, 4, HALF], F32, name="raw%d" % h) for h in range(2)]
         word_table = keep.tile([P, N], U32, name="word_table", align_bytes=64)
         w_flat = w_words[0].rearrange("p n r -> p (n r)")
-        for a, z in zip(LOAD_CUTS[:-1], LOAD_CUTS[1:]):
-            if z == N:
-                load_scales(EARLY + SPARE, N, (nc.sync, nc.sync))
+
+        def load_x(h):
+            nc.sync.dma_start(raws[h][:], x_rows[:, :, h * HALF : (h + 1) * HALF])
+
+        def load_words(a, z):
             nc.sync.dma_start(word_table[:, a:z].bitcast(I32), w_flat[:, 4 * a : 4 * z].bitcast(I32))
 
+        nc.sync.dma_start(offsets[:], offs)
+        load_x(0)
+        for q, queue in zip((0, 2, 1, 3), (nc.sync, nc.sync, nc.scalar, nc.scalar)):
+            queue.dma_start(scale_table[32 * q : 32 * q + 4, :].bitcast(I32), w_scales[0, 4 * q : 4 * q + 4, :].bitcast(I32))
+        nc.sync.dma_start(bias_rows[BIAS_ROW:32, :], b.rearrange("(c p) o -> c (p o)", p=P))
+        warm = keep.tile([P, 1], F32, name="warm")
+        nc.scalar.activation(warm[:], zero[:], GELU)
+        load_words(0, 1408)
+        load_x(1)
+        load_words(1408, N)
+
+        ones = keep.tile([P, P], F32, name="ones")
+        nc.vector.memset(ones[:], 1.0)
+        column = keep.tile([P, P], F32, name="column", align_bytes=64)
+        nc.vector.tensor_tensor_scan(column[:], ones[:], ones[:], -1.0, ALU.mult, ALU.add)
+        turned = keep.tile([P, P], F32, name="turned", align_bytes=64)
+        nc.vector.transpose(turned[:], column[:])
         ident = keep.tile([P, P], F32, name="ident")
-        make_identity(nc, ident[:])
+        for q in range(0, P, 32):
+            nc.vector.tensor_scalar(ident[q : q + 32, :], column[q : q + 32, :], turned[q : q + 32, q : q + 1], None, ALU.is_equal)
 
         def gather(dst, table, a, z):
-            nc.vector.tensor_copy(dst, table[:, 0 : z + SPARE].indirect(offsets[:, a // 16 : z // 16]))
-
-        early = keep.tile([P, EARLY], U8, name="early", align_bytes=64)
-        gather(early[:], scale_table, 0, EARLY)
+            tile, first = dst
+            nc.vector.tensor_copy(tile[:, a - first : z - first], table[:, 0 : z + SPARE].indirect(offsets[:, a // 16 : z // 16]))
 
         x_codes = keep.tile([P, T], U32, name="x_codes", align_bytes=64)
         x_scale = keep.tile([P, T], U8, name="x_scale", align_bytes=64)
-        grouped = [keep.tile([P, HALF, 4], BF16, name="grouped%d" % u, align_bytes=64) for u in range(2)]
+        grouped = [keep.tile([P, HALF, 4], BF16, name="grouped0", align_bytes=64),
+                   reuse.tile([P, HALF, 4], BF16, name="grouped1", align_bytes=64, offset=2048)]
 
         def cast(copy, h, a, z):
-            u = a // HALF
-            copy(grouped[u][:, a - u * HALF : z - u * HALF, 2 * h : 2 * h + 2], raws[h][:, :, a:z].rearrange("p j t -> p t j"))
+            copy(grouped[h][:, a:z, :].rearrange("p (c i) j -> p c j i", i=4), raws[h][:, :, a:z].rearrange("p j (c i) -> p c j i", i=4))
 
-        cast(nc.scalar.copy, 0, 0, HALF)
-        cast(nc.scalar.copy, 0, HALF, 384)
-        cast(nc.vector.tensor_copy, 0, 384, T)
-        cast(nc.vector.tensor_copy, 1, 0, 160)
-        cast(nc.scalar.copy, 1, 160, HALF)
-        cast(nc.scalar.copy, 1, HALF, 416)
-        cast(nc.vector.tensor_copy, 1, 416, T)
-        for u in range(2):
-            cols = slice(u * HALF, (u + 1) * HALF)
-            nc.vector.quantize_mx(out=x_codes[:, cols].bitcast(FP8X4), scales=x_scale[:, cols], in_=grouped[u][:].rearrange("p t j -> p (t j)"))
+        def quantize(h):
+            cols = slice(h * HALF, (h + 1) * HALF)
+            nc.vector.quantize_mx(out=x_codes[:, cols].bitcast(FP8X4), scales=x_scale[:, cols], in_=grouped[h][:].rearrange("p t j -> p (t j)"))
 
         bias_ps = psum_b.tile([P, P], F32, name="bias_ps")
         nc.tensor.transpose(bias_ps[:], bias_rows[:], ident[:])
-        bias = keep.tile([P, S // P], F32, name="bias")
-        nc.scalar.copy(bias[:], bias_ps[:, 0 : S // P])
+        bias = keep.tile([P, TILES], F32, name="bias")
+        nc.scalar.copy(bias[:], bias_ps[:, BIAS_ROW:32])
 
-        def product(t, codes, plane):
-            rows = slice(t * P, (t + 1) * P)
-            cuts = {0: (0, HALF // 2, HALF, T), 1: (0, HALF, T), 2: (0, HALF, T)}.get(t, (0, T))
-            for a, z in zip(cuts[:-1], cuts[1:]):
-                cols = slice(a, z)
-                acc = psum.tile([P, z - a], F32, name="acc")
-                nc.tensor.matmul_mx(out=acc[:], lhsT=codes.bitcast(FP8X4), lhsT_scale=plane,
-                                    rhs=x_codes[:, cols].bitcast(FP8X4), rhs_scale=x_scale[:, cols], start=True, stop=True)
-                y = res.tile([P, z - a], F32, name="y")
-                nc.scalar.activation(y[:], acc[:], GELU, bias=bias[:, t : t + 1])
-                nc.sync.dma_start(out[rows, cols], y[:])
+        codes_a = (reuse.tile([P, 384], U32, name="codes_a", align_bytes=64, offset=0), 0)
+        codes_b = (reuse.tile([P, S - 384], U32, name="codes_b", align_bytes=64, offset=2112), 384)
+        bytes_a = (keep.tile([P, 384], U8, name="bytes_a", align_bytes=64), 0)
+        bytes_b = (reuse.tile([P, 384], U8, name="bytes_b", align_bytes=64, offset=1728), 384)
+        bytes_c = (reuse.tile([P, 256], U8, name="bytes_c", align_bytes=64, offset=0), 768)
 
-        w_codes = reuse.tile([P, S], U32, name="w_codes", align_bytes=64, offset=0)
-        late = keep.tile([P, S - EARLY], U8, name="late", align_bytes=64)
+        def columns(piece, t):
+            tile, first = piece
+            return tile[:, t * P - first : (t + 1) * P - first]
 
-        def tile_product(t):
-            c = t * P
-            product(t, w_codes[:, c : c + P], early[:, c : c + P] if c < EARLY else late[:, c - EARLY : c - EARLY + P])
+        def product(t, a, z):
+            picked = slice(t * P, (t + 1) * P)
+            codes = columns(codes_a if t < 3 else codes_b, t)
+            plane = columns((bytes_a, bytes_b, bytes_c)[t // 3], t)
+            cols = slice(a, z)
+            acc = psum.tile([P, z - a], F32, name="acc")
+            nc.tensor.matmul_mx(out=acc[:], lhsT=codes.bitcast(FP8X4), lhsT_scale=plane,
+                                rhs=x_codes[:, cols].bitcast(FP8X4), rhs_scale=x_scale[:, cols], start=True, stop=True)
+            y = res.tile([P, z - a], F32, name="y")
+            nc.scalar.activation(y[:], acc[:], GELU, bias=bias[:, t : t + 1])
+            nc.sync.dma_start(out[picked, cols], y[:])
 
-        gather(w_codes[:, 0:160], word_table, 0, 160)
-        tile_product(0)
-        gather(w_codes[:, 160:384], word_table, 160, 384)
-        tile_product(1)
-        tile_product(2)
-        gather(w_codes[:, 384:768], word_table, 384, 768)
-        tile_product(3)
-        gather(late[:, 0:256], scale_table, 512, 768)
-        tile_product(4)
-        tile_product(5)
-        gather(late[:, 256:512], scale_table, 768, S)
-        gather(w_codes[:, 768:S], word_table, 768, S)
-        tile_product(6)
-        tile_product(7)
+        def prepare_tokens(h):
+            cast((nc.scalar.copy, nc.vector.tensor_copy)[h], h, 0, HALF)
+            quantize(h)
+
+        gather(bytes_a, scale_table, 0, 384)
+        prepare_tokens(0)
+        gather(codes_a, word_table, 0, 160)
+        product(0, 0, HALF)
+        gather(codes_a, word_table, 160, 384)
+        product(1, 0, HALF)
+        product(2, 0, HALF)
+        prepare_tokens(1)
+        for t in range(3):
+            product(t, HALF, T)
+        gather(bytes_b, scale_table, 384, 768)
+        gather(codes_b, word_table, 384, 640)
+        product(3, 0, T)
+        product(4, 0, T)
+        gather(codes_b, word_table, 640, S)
+        product(5, 0, T)
+        gather(bytes_c, scale_table, 768, S)
+        product(6, 0, T)
+        product(7, 0, T)

@@ -17,7 +17,8 @@ P = 128
 SPARE = N - S
 HALF = T // 2
 TILES = S // P
-BIAS_ROW = 32 - TILES
+EARLY = 640
+VECTOR_SHARE = 128
 
 
 def tile_picked_neuron_lin_gelu_srt_p_kernel(tc, w_words, w_scales, xT, b, offs, out):
@@ -30,35 +31,41 @@ def tile_picked_neuron_lin_gelu_srt_p_kernel(tc, w_words, w_scales, xT, b, offs,
         psum = ctx.enter_context(tc.psum_pool(name="psum", bufs=7))
 
         scale_table = keep.tile([P, N], U8, name="scale_table", align_bytes=64)
-        nc.vector.memset(scale_table[:].bitcast(I32), 0)
+        nc.gpsimd.memset(scale_table[:, 0 : EARLY + SPARE].bitcast(I32), 0)
         zero = keep.tile([P, 1], F32, name="zero")
-        nc.vector.memset(zero[:], 0.0)
+        nc.gpsimd.memset(zero[:], 0.0)
+        nc.gpsimd.memset(scale_table[:, EARLY + SPARE : N].bitcast(I32), 0)
         bias_rows = reuse.tile([P, P], F32, name="bias_rows", align_bytes=64, offset=0)
-        for lo, hi in ((0, BIAS_ROW), (32, 64), (64, P)):
-            nc.gpsimd.memset(bias_rows[lo:hi, :], 0.0)
+        nc.vector.memset(bias_rows[:], 0.0)
 
         offsets = keep.tile([P, S // 16], U16, name="offsets")
         x_rows = xT.rearrange("(p j) t -> p j t", j=4)
-        raws = [keep.tile([P, 4, HALF], F32, name="raw%d" % h) for h in range(2)]
+        low = keep.tile([P, 2, T], F32, name="low")
+        high = [reuse.tile([P, 2, HALF], F32, name="high0", align_bytes=64, offset=2048), reuse.tile([P, 2, HALF], F32, name="high1", align_bytes=64, offset=5760)]
         word_table = keep.tile([P, N], U32, name="word_table", align_bytes=64)
         w_flat = w_words[0].rearrange("p n r -> p (n r)")
-
-        def load_x(h):
-            nc.sync.dma_start(raws[h][:], x_rows[:, :, h * HALF : (h + 1) * HALF])
 
         def load_words(a, z):
             nc.sync.dma_start(word_table[:, a:z].bitcast(I32), w_flat[:, 4 * a : 4 * z].bitcast(I32))
 
         nc.sync.dma_start(offsets[:], offs)
-        load_x(0)
-        for q, queue in zip((0, 2, 1, 3), (nc.sync, nc.sync, nc.scalar, nc.scalar)):
-            queue.dma_start(scale_table[32 * q : 32 * q + 4, :].bitcast(I32), w_scales[0, 4 * q : 4 * q + 4, :].bitcast(I32))
-        nc.sync.dma_start(bias_rows[BIAS_ROW:32, :], b.rearrange("(c p) o -> c (p o)", p=P))
+        nc.sync.dma_start(low[:], x_rows[:, 0:2, :])
+
+        def load_scales(a, z, queues):
+            for q in (0, 3, 2, 1):
+                queues[q % 2].dma_start(scale_table[32 * q : 32 * q + 4, a:z].bitcast(I32), w_scales[0, 4 * q : 4 * q + 4, a:z].bitcast(I32))
+
+        load_scales(0, EARLY + SPARE, (nc.sync, nc.scalar))
         warm = keep.tile([P, 1], F32, name="warm")
         nc.scalar.activation(warm[:], zero[:], GELU)
-        load_words(0, 1408)
-        load_x(1)
-        load_words(1408, N)
+        nc.sync.dma_start(high[0][:], x_rows[:, 2:4, 0:HALF])
+        nc.sync.dma_start(bias_rows[0:TILES, :], b.rearrange("(c p) o -> c (p o)", p=P))
+        load_words(0, 1184)
+        load_words(1184, 1408)
+        nc.sync.dma_start(high[1][:], x_rows[:, 2:4, HALF:T])
+        load_words(1408, 1792)
+        load_scales(EARLY + SPARE, N, (nc.sync, nc.sync))
+        load_words(1792, N)
 
         ones = keep.tile([P, P], F32, name="ones")
         nc.vector.memset(ones[:], 1.0)
@@ -79,60 +86,64 @@ def tile_picked_neuron_lin_gelu_srt_p_kernel(tc, w_words, w_scales, xT, b, offs,
         grouped = [keep.tile([P, HALF, 4], BF16, name="grouped0", align_bytes=64),
                    reuse.tile([P, HALF, 4], BF16, name="grouped1", align_bytes=64, offset=2048)]
 
-        def cast(copy, h, a, z):
-            copy(grouped[h][:, a:z, :].rearrange("p (c i) j -> p c j i", i=4), raws[h][:, :, a:z].rearrange("p j (c i) -> p c j i", i=4))
+        def cast_low(copy, a, z):
+            u = a // HALF
+            copy(grouped[u][:, a - u * HALF : z - u * HALF, 0:2], low[:, :, a:z].rearrange("p j t -> p t j"))
 
-        def quantize(h):
-            cols = slice(h * HALF, (h + 1) * HALF)
-            nc.vector.quantize_mx(out=x_codes[:, cols].bitcast(FP8X4), scales=x_scale[:, cols], in_=grouped[h][:].rearrange("p t j -> p (t j)"))
+        def cast_high(copy, u, a, z):
+            copy(grouped[u][:, a:z, 2:4], high[u][:, :, a:z].rearrange("p j t -> p t j"))
+
+        def quantize(u):
+            cols = slice(u * HALF, (u + 1) * HALF)
+            nc.vector.quantize_mx(out=x_codes[:, cols].bitcast(FP8X4), scales=x_scale[:, cols], in_=grouped[u][:].rearrange("p t j -> p (t j)"))
+
+        bytes_a = (keep.tile([P, EARLY], U8, name="bytes_a", align_bytes=64), 0)
+        cast_low(nc.scalar.copy, 0, HALF)
+        gather(bytes_a, scale_table, 0, EARLY)
+        cast_high(nc.scalar.copy, 0, 0, HALF)
+        cast_low(nc.scalar.copy, HALF, T)
+        quantize(0)
 
         bias_ps = psum_b.tile([P, P], F32, name="bias_ps")
         nc.tensor.transpose(bias_ps[:], bias_rows[:], ident[:])
         bias = keep.tile([P, TILES], F32, name="bias")
-        nc.scalar.copy(bias[:], bias_ps[:, BIAS_ROW:32])
+        nc.scalar.copy(bias[:], bias_ps[:, 0:TILES])
 
         codes_a = (reuse.tile([P, 384], U32, name="codes_a", align_bytes=64, offset=0), 0)
         codes_b = (reuse.tile([P, S - 384], U32, name="codes_b", align_bytes=64, offset=2112), 384)
-        bytes_a = (keep.tile([P, 384], U8, name="bytes_a", align_bytes=64), 0)
-        bytes_b = (reuse.tile([P, 384], U8, name="bytes_b", align_bytes=64, offset=1728), 384)
-        bytes_c = (reuse.tile([P, 256], U8, name="bytes_c", align_bytes=64, offset=0), 768)
+        bytes_b = (reuse.tile([P, S - EARLY], U8, name="bytes_b", align_bytes=64, offset=2112 - (S - EARLY)), EARLY)
 
         def columns(piece, t):
             tile, first = piece
             return tile[:, t * P - first : (t + 1) * P - first]
 
-        def product(t, a, z):
+        def product(t, a, z, y=None):
             picked = slice(t * P, (t + 1) * P)
             codes = columns(codes_a if t < 3 else codes_b, t)
-            plane = columns((bytes_a, bytes_b, bytes_c)[t // 3], t)
+            plane = columns(bytes_a if t * P < EARLY else bytes_b, t)
             cols = slice(a, z)
             acc = psum.tile([P, z - a], F32, name="acc")
             nc.tensor.matmul_mx(out=acc[:], lhsT=codes.bitcast(FP8X4), lhsT_scale=plane,
                                 rhs=x_codes[:, cols].bitcast(FP8X4), rhs_scale=x_scale[:, cols], start=True, stop=True)
-            y = res.tile([P, z - a], F32, name="y")
+            if y is None:
+                y = res.tile([P, z - a], F32, name="y")
             nc.scalar.activation(y[:], acc[:], GELU, bias=bias[:, t : t + 1])
             nc.sync.dma_start(out[picked, cols], y[:])
 
-        def prepare_tokens(h):
-            cast((nc.scalar.copy, nc.vector.tensor_copy)[h], h, 0, HALF)
-            quantize(h)
-
-        gather(bytes_a, scale_table, 0, 384)
-        prepare_tokens(0)
         gather(codes_a, word_table, 0, 160)
-        product(0, 0, HALF)
         gather(codes_a, word_table, 160, 384)
-        product(1, 0, HALF)
-        product(2, 0, HALF)
-        prepare_tokens(1)
+        cast_high(nc.scalar.copy, 1, VECTOR_SHARE, HALF)
+        cast_high(nc.vector.tensor_copy, 1, 0, VECTOR_SHARE)
+        for t in range(3):
+            product(t, 0, HALF, reuse.tile([P, HALF], F32, name="y_first%d" % t, align_bytes=64, offset=4800 + 1024 * t))
+        quantize(1)
         for t in range(3):
             product(t, HALF, T)
-        gather(bytes_b, scale_table, 384, 768)
-        gather(codes_b, word_table, 384, 640)
+        gather(codes_b, word_table, 384, 768)
         product(3, 0, T)
         product(4, 0, T)
-        gather(codes_b, word_table, 640, S)
+        gather(bytes_b, scale_table, EARLY, S)
         product(5, 0, T)
-        gather(bytes_c, scale_table, 768, S)
+        gather(codes_b, word_table, 768, S)
         product(6, 0, T)
         product(7, 0, T)

@@ -35,7 +35,7 @@ def tile_picked_neuron_lin_gelu_srt_p_kernel(tc, w_words, w_scales, xT, b, offs,
         zero = keep.tile([P, 1], F32, name="zero")
         nc.gpsimd.memset(zero[:], 0.0)
         nc.gpsimd.memset(scale_table[:, EARLY + SPARE : N].bitcast(I32), 0)
-        bias_rows = reuse.tile([P, P], F32, name="bias_rows", align_bytes=64, offset=0)
+        bias_rows = keep.tile([P, P], F32, name="bias_rows", align_bytes=64)
         nc.vector.memset(bias_rows[:], 0.0)
 
         offsets = keep.tile([P, S // 16], U16, name="offsets")
@@ -48,8 +48,8 @@ def tile_picked_neuron_lin_gelu_srt_p_kernel(tc, w_words, w_scales, xT, b, offs,
         def load_words(a, z):
             nc.sync.dma_start(word_table[:, a:z].bitcast(I32), w_flat[:, 4 * a : 4 * z].bitcast(I32))
 
-        nc.sync.dma_start(offsets[:], offs)
         nc.sync.dma_start(low[:], x_rows[:, 0:2, :])
+        nc.sync.dma_start(offsets[:], offs)
 
         def load_scales(a, z, queues):
             for q in (0, 3, 2, 1):
@@ -59,8 +59,8 @@ def tile_picked_neuron_lin_gelu_srt_p_kernel(tc, w_words, w_scales, xT, b, offs,
         warm = keep.tile([P, 1], F32, name="warm")
         nc.scalar.activation(warm[:], zero[:], GELU)
         nc.sync.dma_start(high[0][:], x_rows[:, 2:4, 0:HALF])
-        nc.sync.dma_start(bias_rows[0:TILES, :], b.rearrange("(c p) o -> c (p o)", p=P))
         load_words(0, 1184)
+        nc.sync.dma_start(bias_rows[0:TILES, :], b.rearrange("(c p) o -> c (p o)", p=P))
         load_words(1184, 1408)
         nc.sync.dma_start(high[1][:], x_rows[:, 2:4, HALF:T])
         load_words(1408, 1792)
@@ -104,14 +104,14 @@ def tile_picked_neuron_lin_gelu_srt_p_kernel(tc, w_words, w_scales, xT, b, offs,
         cast_low(nc.scalar.copy, HALF, T)
         quantize(0)
 
-        bias_ps = psum_b.tile([P, P], F32, name="bias_ps")
+        bias_ps = psum_b.tile([P, P], F32, name="bias_ps", tag="first_bank")
         nc.tensor.transpose(bias_ps[:], bias_rows[:], ident[:])
         bias = keep.tile([P, TILES], F32, name="bias")
         nc.scalar.copy(bias[:], bias_ps[:, 0:TILES])
 
-        codes_a = (reuse.tile([P, 384], U32, name="codes_a", align_bytes=64, offset=0), 0)
-        codes_b = (reuse.tile([P, S - 384], U32, name="codes_b", align_bytes=64, offset=2112), 384)
-        bytes_b = (reuse.tile([P, S - EARLY], U8, name="bytes_b", align_bytes=64, offset=2112 - (S - EARLY)), EARLY)
+        codes_a = (keep.tile([P, 384], U32, name="codes_a", align_bytes=64), 0)
+        codes_b = (keep.tile([P, S - 384], U32, name="codes_b", align_bytes=64), 384)
+        bytes_b = (keep.tile([P, S - EARLY], U8, name="bytes_b", align_bytes=64), EARLY)
 
         def columns(piece, t):
             tile, first = piece
@@ -122,7 +122,10 @@ def tile_picked_neuron_lin_gelu_srt_p_kernel(tc, w_words, w_scales, xT, b, offs,
             codes = columns(codes_a if t < 3 else codes_b, t)
             plane = columns(bytes_a if t * P < EARLY else bytes_b, t)
             cols = slice(a, z)
-            acc = psum.tile([P, z - a], F32, name="acc")
+            if (t, a) == (0, 0):
+                acc = psum_b.tile([P, z - a], F32, name="first_acc", tag="first_bank")
+            else:
+                acc = psum.tile([P, z - a], F32, name="acc")
             nc.tensor.matmul_mx(out=acc[:], lhsT=codes.bitcast(FP8X4), lhsT_scale=plane,
                                 rhs=x_codes[:, cols].bitcast(FP8X4), rhs_scale=x_scale[:, cols], start=True, stop=True)
             if y is None:

@@ -18,6 +18,7 @@ SPARE = N - S
 HALF = T // 2
 TILES = S // P
 EARLY = 640
+SPLIT = 3
 VECTOR_SHARE = 128
 
 
@@ -41,7 +42,7 @@ def tile_picked_neuron_lin_gelu_srt_p_kernel(tc, w_words, w_scales, xT, b, offs,
         offsets = keep.tile([P, S // 16], U16, name="offsets")
         x_rows = xT.rearrange("(p j) t -> p j t", j=4)
         low = keep.tile([P, 2, T], F32, name="low")
-        high = [reuse.tile([P, 2, HALF], F32, name="high0", align_bytes=64, offset=2048), reuse.tile([P, 2, HALF], F32, name="high1", align_bytes=64, offset=5760)]
+        high = [reuse.tile([P, 2, HALF], F32, name="high0", align_bytes=64, offset=1024), reuse.tile([P, 2, HALF], F32, name="high1", align_bytes=64, offset=5760)]
         word_table = keep.tile([P, N], U32, name="word_table", align_bytes=64)
         w_flat = w_words[0].rearrange("p n r -> p (n r)")
 
@@ -63,9 +64,9 @@ def tile_picked_neuron_lin_gelu_srt_p_kernel(tc, w_words, w_scales, xT, b, offs,
         nc.sync.dma_start(bias_rows[0:TILES, :], b.rearrange("(c p) o -> c (p o)", p=P))
         load_words(1184, 1408)
         nc.sync.dma_start(high[1][:], x_rows[:, 2:4, HALF:T])
-        load_words(1408, 1792)
+        load_words(1408, 1664)
         load_scales(EARLY + SPARE, N, (nc.sync, nc.sync))
-        load_words(1792, N)
+        load_words(1664, N)
 
         ones = keep.tile([P, P], F32, name="ones")
         nc.vector.memset(ones[:], 1.0)
@@ -77,18 +78,17 @@ def tile_picked_neuron_lin_gelu_srt_p_kernel(tc, w_words, w_scales, xT, b, offs,
         for q in range(0, P, 32):
             nc.vector.tensor_scalar(ident[q : q + 32, :], column[q : q + 32, :], turned[q : q + 32, q : q + 1], None, ALU.is_equal)
 
-        def gather(dst, table, a, z):
+        def gather(dst, table, a, z, window=None):
             tile, first = dst
-            nc.vector.tensor_copy(tile[:, a - first : z - first], table[:, 0 : z + SPARE].indirect(offsets[:, a // 16 : z // 16]))
+            nc.vector.tensor_copy(tile[:, a - first : z - first], table[:, 0 : window or z + SPARE].indirect(offsets[:, a // 16 : z // 16]))
 
         x_codes = keep.tile([P, T], U32, name="x_codes", align_bytes=64)
         x_scale = keep.tile([P, T], U8, name="x_scale", align_bytes=64)
         grouped = [keep.tile([P, HALF, 4], BF16, name="grouped0", align_bytes=64),
                    reuse.tile([P, HALF, 4], BF16, name="grouped1", align_bytes=64, offset=2048)]
 
-        def cast_low(copy, a, z):
-            u = a // HALF
-            copy(grouped[u][:, a - u * HALF : z - u * HALF, 0:2], low[:, :, a:z].rearrange("p j t -> p t j"))
+        def cast_low(copy, u):
+            copy(grouped[u][:, :, 0:2], low[:, :, u * HALF : (u + 1) * HALF].rearrange("p j t -> p t j"))
 
         def cast_high(copy, u, a, z):
             copy(grouped[u][:, a:z, 2:4], high[u][:, :, a:z].rearrange("p j t -> p t j"))
@@ -98,10 +98,10 @@ def tile_picked_neuron_lin_gelu_srt_p_kernel(tc, w_words, w_scales, xT, b, offs,
             nc.vector.quantize_mx(out=x_codes[:, cols].bitcast(FP8X4), scales=x_scale[:, cols], in_=grouped[u][:].rearrange("p t j -> p (t j)"))
 
         bytes_a = (keep.tile([P, EARLY], U8, name="bytes_a", align_bytes=64), 0)
-        cast_low(nc.scalar.copy, 0, HALF)
+        cast_low(nc.scalar.copy, 0)
         gather(bytes_a, scale_table, 0, EARLY)
         cast_high(nc.scalar.copy, 0, 0, HALF)
-        cast_low(nc.scalar.copy, HALF, T)
+        cast_low(nc.scalar.copy, 1)
         quantize(0)
 
         bias_ps = psum_b.tile([P, P], F32, name="bias_ps", tag="first_bank")
@@ -109,8 +109,8 @@ def tile_picked_neuron_lin_gelu_srt_p_kernel(tc, w_words, w_scales, xT, b, offs,
         bias = keep.tile([P, TILES], F32, name="bias")
         nc.scalar.copy(bias[:], bias_ps[:, 0:TILES])
 
-        codes_a = (keep.tile([P, 384], U32, name="codes_a", align_bytes=64), 0)
-        codes_b = (keep.tile([P, S - 384], U32, name="codes_b", align_bytes=64), 384)
+        codes_a = (reuse.tile([P, SPLIT * P], U32, name="codes_a", align_bytes=64, offset=0), 0)
+        codes_b = (keep.tile([P, S - SPLIT * P], U32, name="codes_b", align_bytes=64), SPLIT * P)
         bytes_b = (keep.tile([P, S - EARLY], U8, name="bytes_b", align_bytes=64), EARLY)
 
         def columns(piece, t):
@@ -119,7 +119,7 @@ def tile_picked_neuron_lin_gelu_srt_p_kernel(tc, w_words, w_scales, xT, b, offs,
 
         def product(t, a, z, y=None):
             picked = slice(t * P, (t + 1) * P)
-            codes = columns(codes_a if t < 3 else codes_b, t)
+            codes = columns(codes_a if t < SPLIT else codes_b, t)
             plane = columns(bytes_a if t * P < EARLY else bytes_b, t)
             cols = slice(a, z)
             if (t, a) == (0, 0):
@@ -134,19 +134,18 @@ def tile_picked_neuron_lin_gelu_srt_p_kernel(tc, w_words, w_scales, xT, b, offs,
             nc.sync.dma_start(out[picked, cols], y[:])
 
         gather(codes_a, word_table, 0, 160)
-        gather(codes_a, word_table, 160, 384)
+        gather(codes_a, word_table, 160, SPLIT * P)
         cast_high(nc.scalar.copy, 1, VECTOR_SHARE, HALF)
         cast_high(nc.vector.tensor_copy, 1, 0, VECTOR_SHARE)
-        for t in range(3):
+        for t in range(SPLIT):
             product(t, 0, HALF, reuse.tile([P, HALF], F32, name="y_first%d" % t, align_bytes=64, offset=4800 + 1024 * t))
         quantize(1)
-        for t in range(3):
+        for t in range(SPLIT):
             product(t, HALF, T)
-        gather(codes_b, word_table, 384, 768)
+        gather(codes_b, word_table, 384, 640)
         product(3, 0, T)
         product(4, 0, T)
         gather(bytes_b, scale_table, EARLY, S)
-        product(5, 0, T)
-        gather(codes_b, word_table, 768, S)
-        product(6, 0, T)
-        product(7, 0, T)
+        for t in range(5, TILES):
+            gather(codes_b, word_table, t * P, (t + 1) * P, N)
+            product(t, 0, T)

@@ -32,10 +32,9 @@ def tile_picked_neuron_lin_gelu_srt_p_kernel(tc, w_words, w_scales, xT, b, offs,
         psum = ctx.enter_context(tc.psum_pool(name="psum", bufs=7))
 
         scale_table = keep.tile([P, N], U8, name="scale_table", align_bytes=64)
-        nc.gpsimd.memset(scale_table[:, 0 : EARLY + SPARE].bitcast(I32), 0)
+        nc.gpsimd.memset(scale_table[:].bitcast(I32), 0)
         zero = keep.tile([P, 1], F32, name="zero")
         nc.gpsimd.memset(zero[:], 0.0)
-        nc.gpsimd.memset(scale_table[:, EARLY + SPARE : N].bitcast(I32), 0)
         bias_rows = keep.tile([P, P], F32, name="bias_rows", align_bytes=64)
         nc.vector.memset(bias_rows[:], 0.0)
 
@@ -51,12 +50,8 @@ def tile_picked_neuron_lin_gelu_srt_p_kernel(tc, w_words, w_scales, xT, b, offs,
 
         nc.sync.dma_start(low[:], x_rows[:, 0:2, :])
         nc.sync.dma_start(offsets[:], offs)
-
-        def load_scales(a, z, queues):
-            for q in (0, 3, 2, 1):
-                queues[q % 2].dma_start(scale_table[32 * q : 32 * q + 4, a:z].bitcast(I32), w_scales[0, 4 * q : 4 * q + 4, a:z].bitcast(I32))
-
-        load_scales(0, EARLY + SPARE, (nc.sync, nc.scalar))
+        for r in range(4):
+            (nc.sync, nc.scalar)[r % 2].dma_start(scale_table[r:P:32, :].bitcast(I32), w_scales[0, r:16:4, :].bitcast(I32))
         warm = keep.tile([P, 1], F32, name="warm")
         nc.scalar.activation(warm[:], zero[:], GELU)
         nc.sync.dma_start(high[0][:], x_rows[:, 2:4, 0:HALF])
@@ -64,9 +59,7 @@ def tile_picked_neuron_lin_gelu_srt_p_kernel(tc, w_words, w_scales, xT, b, offs,
         nc.sync.dma_start(bias_rows[0:TILES, :], b.rearrange("(c p) o -> c (p o)", p=P))
         load_words(1184, 1408)
         nc.sync.dma_start(high[1][:], x_rows[:, 2:4, HALF:T])
-        load_words(1408, 1664)
-        load_scales(EARLY + SPARE, N, (nc.sync, nc.sync))
-        load_words(1664, N)
+        load_words(1408, N)
 
         ones = keep.tile([P, P], F32, name="ones")
         nc.vector.memset(ones[:], 1.0)
@@ -111,7 +104,7 @@ def tile_picked_neuron_lin_gelu_srt_p_kernel(tc, w_words, w_scales, xT, b, offs,
 
         codes_a = (reuse.tile([P, SPLIT * P], U32, name="codes_a", align_bytes=64, offset=0), 0)
         codes_b = (keep.tile([P, S - SPLIT * P], U32, name="codes_b", align_bytes=64), SPLIT * P)
-        bytes_b = (keep.tile([P, S - EARLY], U8, name="bytes_b", align_bytes=64), EARLY)
+        bytes_b = (reuse.tile([P, S - EARLY], U8, name="bytes_b", align_bytes=64, offset=2048), EARLY)
 
         def columns(piece, t):
             tile, first = piece

@@ -19,7 +19,8 @@ HALF = T // 2
 TILES = S // P
 EARLY = 640
 SPLIT = 3
-VECTOR_SHARE = 128
+QUARTER = T // 4
+VECTOR_SHARES = (48, 80)
 
 
 def tile_picked_neuron_lin_gelu_srt_p_kernel(tc, w_words, w_scales, xT, b, offs, out):
@@ -86,16 +87,18 @@ def tile_picked_neuron_lin_gelu_srt_p_kernel(tc, w_words, w_scales, xT, b, offs,
         def cast_high(copy, u, a, z):
             copy(grouped[u][:, a:z, 2:4], high[u][:, :, a:z].rearrange("p j t -> p t j"))
 
-        def quantize(u):
-            cols = slice(u * HALF, (u + 1) * HALF)
-            nc.vector.quantize_mx(out=x_codes[:, cols].bitcast(FP8X4), scales=x_scale[:, cols], in_=grouped[u][:].rearrange("p t j -> p (t j)"))
+        def quantize(u, a):
+            cols = slice(u * HALF + a, u * HALF + a + QUARTER)
+            nc.vector.quantize_mx(out=x_codes[:, cols].bitcast(FP8X4), scales=x_scale[:, cols], in_=grouped[u][:, a : a + QUARTER, :].rearrange("p t j -> p (t j)"))
 
         bytes_a = (keep.tile([P, EARLY], U8, name="bytes_a", align_bytes=64), 0)
         cast_low(nc.scalar.copy, 0)
         gather(bytes_a, scale_table, 0, EARLY)
-        cast_high(nc.scalar.copy, 0, 0, HALF)
+        for a in (0, QUARTER):
+            cast_high(nc.scalar.copy, 0, a, a + QUARTER)
         cast_low(nc.scalar.copy, 1)
-        quantize(0)
+        for a in (0, QUARTER):
+            quantize(0, a)
 
         bias_ps = psum_b.tile([P, P], F32, name="bias_ps", tag="first_bank")
         nc.tensor.transpose(bias_ps[:], bias_rows[:], ident[:])
@@ -119,8 +122,10 @@ def tile_picked_neuron_lin_gelu_srt_p_kernel(tc, w_words, w_scales, xT, b, offs,
                 acc = psum_b.tile([P, z - a], F32, name="first_acc", tag="first_bank")
             else:
                 acc = psum.tile([P, z - a], F32, name="acc")
-            nc.tensor.matmul_mx(out=acc[:], lhsT=codes.bitcast(FP8X4), lhsT_scale=plane,
-                                rhs=x_codes[:, cols].bitcast(FP8X4), rhs_scale=x_scale[:, cols], start=True, stop=True)
+            width = QUARTER if (t, a) == (0, HALF) else z - a
+            for c in range(a, z, width):
+                nc.tensor.matmul_mx(out=acc[:, c - a : c - a + width], lhsT=codes.bitcast(FP8X4), lhsT_scale=plane,
+                                    rhs=x_codes[:, c : c + width].bitcast(FP8X4), rhs_scale=x_scale[:, c : c + width], start=True, stop=True)
             if y is None:
                 y = res.tile([P, z - a], F32, name="y")
             nc.scalar.activation(y[:], acc[:], GELU, bias=bias[:, t : t + 1])
@@ -128,11 +133,13 @@ def tile_picked_neuron_lin_gelu_srt_p_kernel(tc, w_words, w_scales, xT, b, offs,
 
         gather(codes_a, word_table, 0, 160)
         gather(codes_a, word_table, 160, SPLIT * P)
-        cast_high(nc.scalar.copy, 1, VECTOR_SHARE, HALF)
-        cast_high(nc.vector.tensor_copy, 1, 0, VECTOR_SHARE)
+        for a, share in zip((0, QUARTER), VECTOR_SHARES):
+            cast_high(nc.scalar.copy, 1, a + share, a + QUARTER)
+            cast_high(nc.vector.tensor_copy, 1, a, a + share)
         for t in range(SPLIT):
             product(t, 0, HALF, reuse.tile([P, HALF], F32, name="y_first%d" % t, align_bytes=64, offset=4800 + 1024 * t))
-        quantize(1)
+        for a in (0, QUARTER):
+            quantize(1, a)
         for t in range(SPLIT):
             product(t, HALF, T)
         gather(codes_b, word_table, 384, 640)

@@ -118,17 +118,19 @@ def tile_picked_neuron_lin_gelu_srt_p_kernel(tc, w_words, w_scales, xT, b, offs,
             codes = columns(codes_a if t < SPLIT else codes_b, t)
             plane = columns(bytes_a if t * P < EARLY else bytes_b, t)
             cols = slice(a, z)
-            if (t, a) == (0, 0):
-                acc = psum_b.tile([P, z - a], F32, name="first_acc", tag="first_bank")
-            else:
-                acc = psum.tile([P, z - a], F32, name="acc")
-            width = QUARTER if (t, a) == (0, HALF) else z - a
-            for c in range(a, z, width):
-                nc.tensor.matmul_mx(out=acc[:, c - a : c - a + width], lhsT=codes.bitcast(FP8X4), lhsT_scale=plane,
-                                    rhs=x_codes[:, c : c + width].bitcast(FP8X4), rhs_scale=x_scale[:, c : c + width], start=True, stop=True)
             if y is None:
                 y = res.tile([P, z - a], F32, name="y")
-            nc.scalar.activation(y[:], acc[:], GELU, bias=bias[:, t : t + 1])
+            piece = HALF if t == SPLIT else z - a
+            for first in range(a, z, piece):
+                if (t, a) == (0, 0):
+                    acc = psum_b.tile([P, piece], F32, name="first_acc", tag="first_bank")
+                else:
+                    acc = psum.tile([P, piece], F32, name="acc")
+                width = QUARTER if (t, a) == (0, HALF) else piece
+                for c in range(first, first + piece, width):
+                    nc.tensor.matmul_mx(out=acc[:, c - first : c - first + width], lhsT=codes.bitcast(FP8X4), lhsT_scale=plane,
+                                        rhs=x_codes[:, c : c + width].bitcast(FP8X4), rhs_scale=x_scale[:, c : c + width], start=True, stop=True)
+                nc.scalar.activation(y[:, first - a : first - a + piece], acc[:], GELU, bias=bias[:, t : t + 1])
             nc.sync.dma_start(out[picked, cols], y[:])
 
         gather(codes_a, word_table, 0, 160)
@@ -142,9 +144,9 @@ def tile_picked_neuron_lin_gelu_srt_p_kernel(tc, w_words, w_scales, xT, b, offs,
             quantize(1, a)
         for t in range(SPLIT):
             product(t, HALF, T)
-        gather(codes_b, word_table, 384, 640)
-        product(3, 0, T)
-        product(4, 0, T)
+        for t in (3, 4):
+            gather(codes_b, word_table, t * P, (t + 1) * P, N)
+            product(t, 0, T)
         gather(bytes_b, scale_table, EARLY, S)
         for t in range(5, TILES):
             gather(codes_b, word_table, t * P, (t + 1) * P, N)

@@ -16,11 +16,11 @@ GELU = mybir.ActivationFunctionType.Gelu_apprx_tanh
 P = 128
 SPARE = N - S
 HALF = T // 2
-TILES = S // P
-EARLY = 640
-SPLIT = 3
 QUARTER = T // 4
-VECTOR_SHARES = (48, 80)
+TILES = S // P
+SPLIT = 5
+EARLY = SPLIT * P
+WORD_CUTS = (0, 160, 384, EARLY)
 
 
 def tile_picked_neuron_lin_gelu_srt_p_kernel(tc, w_words, w_scales, xT, b, offs, out):
@@ -28,39 +28,43 @@ def tile_picked_neuron_lin_gelu_srt_p_kernel(tc, w_words, w_scales, xT, b, offs,
     with ExitStack() as ctx:
         keep = ctx.enter_context(tc.tile_pool(name="keep", bufs=1))
         reuse = ctx.enter_context(tc.tile_pool(name="reuse", bufs=1))
-        res = ctx.enter_context(tc.tile_pool(name="res", bufs=12))
+        res = ctx.enter_context(tc.tile_pool(name="res", bufs=13))
         psum_b = ctx.enter_context(tc.psum_pool(name="psum_b", bufs=1))
-        psum = ctx.enter_context(tc.psum_pool(name="psum", bufs=7))
+        psum = ctx.enter_context(tc.psum_pool(name="psum", bufs=6))
 
         scale_table = keep.tile([P, N], U8, name="scale_table", align_bytes=64)
-        nc.gpsimd.memset(scale_table[:].bitcast(I32), 0)
+        nc.vector.memset(scale_table[:].bitcast(I32), 0)
         zero = keep.tile([P, 1], F32, name="zero")
-        nc.gpsimd.memset(zero[:], 0.0)
-        bias_rows = keep.tile([P, P], F32, name="bias_rows", align_bytes=64)
+        nc.vector.memset(zero[:], 0.0)
+        bias_rows = keep.tile([P, 2, P], F32, name="bias_rows", align_bytes=64)
         nc.vector.memset(bias_rows[:], 0.0)
 
         offsets = keep.tile([P, S // 16], U16, name="offsets")
         x_rows = xT.rearrange("(p j) t -> p j t", j=4)
-        low = keep.tile([P, 2, T], F32, name="low")
-        high = [reuse.tile([P, 2, HALF], F32, name="high0", align_bytes=64, offset=1024), reuse.tile([P, 2, HALF], F32, name="high1", align_bytes=64, offset=5760)]
+        raw = [[keep.tile([P, 2, HALF], F32, name="raw%d%d" % (u, e), align_bytes=64) for e in range(2)] for u in range(2)]
         word_table = keep.tile([P, N], U32, name="word_table", align_bytes=64)
         w_flat = w_words[0].rearrange("p n r -> p (n r)")
 
         def load_words(a, z):
             nc.sync.dma_start(word_table[:, a:z].bitcast(I32), w_flat[:, 4 * a : 4 * z].bitcast(I32))
 
-        nc.sync.dma_start(low[:], x_rows[:, 0:2, :])
+        def load_x(u, e):
+            nc.sync.dma_start(raw[u][e][:], x_rows[:, 2 * e : 2 * e + 2, u * HALF : (u + 1) * HALF])
+
+        load_x(0, 0)
         nc.sync.dma_start(offsets[:], offs)
         for r in range(4):
             (nc.sync, nc.scalar)[r % 2].dma_start(scale_table[r:P:32, :].bitcast(I32), w_scales[0, r:16:4, :].bitcast(I32))
         warm = keep.tile([P, 1], F32, name="warm")
         nc.scalar.activation(warm[:], zero[:], GELU)
-        nc.sync.dma_start(high[0][:], x_rows[:, 2:4, 0:HALF])
-        load_words(0, 1184)
-        nc.sync.dma_start(bias_rows[0:TILES, :], b.rearrange("(c p) o -> c (p o)", p=P))
-        load_words(1184, 1408)
-        nc.sync.dma_start(high[1][:], x_rows[:, 2:4, HALF:T])
-        load_words(1408, N)
+        load_x(0, 1)
+        load_words(0, WORD_CUTS[1] + SPARE)
+        nc.sync.dma_start(bias_rows[0 : TILES // 2, :, :], b.rearrange("(h c p) o -> c h (p o)", h=2, p=P))
+        for a, z in zip(WORD_CUTS[1:], WORD_CUTS[2:]):
+            load_words(a + SPARE, z + SPARE)
+        load_x(1, 0)
+        load_x(1, 1)
+        load_words(EARLY + SPARE, N)
 
         ones = keep.tile([P, P], F32, name="ones")
         nc.vector.memset(ones[:], 1.0)
@@ -79,75 +83,65 @@ def tile_picked_neuron_lin_gelu_srt_p_kernel(tc, w_words, w_scales, xT, b, offs,
         x_codes = keep.tile([P, T], U32, name="x_codes", align_bytes=64)
         x_scale = keep.tile([P, T], U8, name="x_scale", align_bytes=64)
         grouped = [keep.tile([P, HALF, 4], BF16, name="grouped0", align_bytes=64),
-                   reuse.tile([P, HALF, 4], BF16, name="grouped1", align_bytes=64, offset=2048)]
+                   reuse.tile([P, HALF, 4], BF16, name="grouped1", align_bytes=64, offset=0)]
 
-        def cast_low(copy, u):
-            copy(grouped[u][:, :, 0:2], low[:, :, u * HALF : (u + 1) * HALF].rearrange("p j t -> p t j"))
-
-        def cast_high(copy, u, a, z):
-            copy(grouped[u][:, a:z, 2:4], high[u][:, :, a:z].rearrange("p j t -> p t j"))
+        def cast(copy, u, e, a, z):
+            copy(grouped[u][:, a:z, 2 * e : 2 * e + 2], raw[u][e][:, :, a:z].rearrange("p j t -> p t j"))
 
         def quantize(u, a):
             cols = slice(u * HALF + a, u * HALF + a + QUARTER)
             nc.vector.quantize_mx(out=x_codes[:, cols].bitcast(FP8X4), scales=x_scale[:, cols], in_=grouped[u][:, a : a + QUARTER, :].rearrange("p t j -> p (t j)"))
 
         bytes_a = (keep.tile([P, EARLY], U8, name="bytes_a", align_bytes=64), 0)
-        cast_low(nc.scalar.copy, 0)
+        cast(nc.scalar.copy, 0, 0, 0, HALF)
         gather(bytes_a, scale_table, 0, EARLY)
         for a in (0, QUARTER):
-            cast_high(nc.scalar.copy, 0, a, a + QUARTER)
-        cast_low(nc.scalar.copy, 1)
+            cast(nc.scalar.copy, 0, 1, a, a + QUARTER)
         for a in (0, QUARTER):
             quantize(0, a)
 
-        bias_ps = psum_b.tile([P, P], F32, name="bias_ps", tag="first_bank")
-        nc.tensor.transpose(bias_ps[:], bias_rows[:], ident[:])
-        bias = keep.tile([P, TILES], F32, name="bias")
-        nc.scalar.copy(bias[:], bias_ps[:, 0:TILES])
+        bias_ps = psum_b.tile([P, P], F32, name="bias_ps")
+        nc.tensor.transpose(bias_ps[:], bias_rows[:, 0, :], ident[:])
+        first_bank = psum_b.tile([P, P + HALF], F32, name="first_bank")
+        nc.tensor.transpose(first_bank[:, 0:P], bias_rows[:, 1, :], ident[:])
+        bias = [keep.tile([P, TILES // 2], F32, name="bias%d" % h) for h in range(2)]
+        nc.scalar.copy(bias[0][:], bias_ps[:, 0 : TILES // 2])
 
-        codes_a = (reuse.tile([P, SPLIT * P], U32, name="codes_a", align_bytes=64, offset=0), 0)
-        codes_b = (keep.tile([P, S - SPLIT * P], U32, name="codes_b", align_bytes=64), SPLIT * P)
-        bytes_b = (reuse.tile([P, S - EARLY], U8, name="bytes_b", align_bytes=64, offset=2048), EARLY)
+        codes_a = (keep.tile([P, EARLY], U32, name="codes_a", align_bytes=64), 0)
+        bytes_b = (reuse.tile([P, S - EARLY], U8, name="bytes_b", align_bytes=64, offset=0), EARLY)
+        codes_b = (reuse.tile([P, S - EARLY], U32, name="codes_b", align_bytes=64, offset=S - EARLY), EARLY)
 
         def columns(piece, t):
             tile, first = piece
             return tile[:, t * P - first : (t + 1) * P - first]
 
-        def product(t, a, z, y=None):
+        def product(t, a, z):
             picked = slice(t * P, (t + 1) * P)
             codes = columns(codes_a if t < SPLIT else codes_b, t)
-            plane = columns(bytes_a if t * P < EARLY else bytes_b, t)
-            cols = slice(a, z)
-            if y is None:
-                y = res.tile([P, z - a], F32, name="y")
-            piece = HALF if t == SPLIT else z - a
-            for first in range(a, z, piece):
-                if (t, a) == (0, 0):
-                    acc = psum_b.tile([P, piece], F32, name="first_acc", tag="first_bank")
-                else:
-                    acc = psum.tile([P, piece], F32, name="acc")
-                width = QUARTER if (t, a) == (0, HALF) else piece
-                for c in range(first, first + piece, width):
-                    nc.tensor.matmul_mx(out=acc[:, c - first : c - first + width], lhsT=codes.bitcast(FP8X4), lhsT_scale=plane,
-                                        rhs=x_codes[:, c : c + width].bitcast(FP8X4), rhs_scale=x_scale[:, c : c + width], start=True, stop=True)
-                nc.scalar.activation(y[:, first - a : first - a + piece], acc[:], GELU, bias=bias[:, t : t + 1])
-            nc.sync.dma_start(out[picked, cols], y[:])
+            plane = columns(bytes_a if t < SPLIT else bytes_b, t)
+            y = res.tile([P, z - a], F32, name="y")
+            acc = first_bank[:, P:] if (t, a) == (0, 0) else psum.tile([P, z - a], F32, name="acc")[:]
+            width = QUARTER if (t, a) == (0, HALF) else z - a
+            for c in range(a, z, width):
+                nc.tensor.matmul_mx(out=acc[:, c - a : c - a + width], lhsT=codes.bitcast(FP8X4), lhsT_scale=plane,
+                                    rhs=x_codes[:, c : c + width].bitcast(FP8X4), rhs_scale=x_scale[:, c : c + width], start=True, stop=True)
+            nc.scalar.activation(y[:], acc, GELU, bias=bias[t // 4][:, t % 4 : t % 4 + 1])
+            nc.sync.dma_start(out[picked, a:z], y[:])
 
-        gather(codes_a, word_table, 0, 160)
-        gather(codes_a, word_table, 160, SPLIT * P)
-        for a, share in zip((0, QUARTER), VECTOR_SHARES):
-            cast_high(nc.scalar.copy, 1, a + share, a + QUARTER)
-            cast_high(nc.vector.tensor_copy, 1, a, a + share)
+        for a, z in zip(WORD_CUTS, WORD_CUTS[1:]):
+            gather(codes_a, word_table, a, z)
         for t in range(SPLIT):
-            product(t, 0, HALF, reuse.tile([P, HALF], F32, name="y_first%d" % t, align_bytes=64, offset=4800 + 1024 * t))
+            product(t, 0, HALF)
+            if t == 0:
+                nc.scalar.copy(bias[1][:], first_bank[:, 0 : TILES // 2])
+        cast(nc.vector.tensor_copy, 1, 0, 0, HALF)
+        for a in (0, QUARTER):
+            cast(nc.vector.tensor_copy, 1, 1, a, a + QUARTER)
         for a in (0, QUARTER):
             quantize(1, a)
         for t in range(SPLIT):
             product(t, HALF, T)
-        for t in (3, 4):
-            gather(codes_b, word_table, t * P, (t + 1) * P, N)
-            product(t, 0, T)
         gather(bytes_b, scale_table, EARLY, S)
-        for t in range(5, TILES):
+        for t in range(SPLIT, TILES):
             gather(codes_b, word_table, t * P, (t + 1) * P, N)
             product(t, 0, T)

@@ -28,7 +28,7 @@ def tile_picked_neuron_lin_gelu_srt_p_kernel(tc, w_words, w_scales, xT, b, offs,
     with ExitStack() as ctx:
         keep = ctx.enter_context(tc.tile_pool(name="keep", bufs=1))
         reuse = ctx.enter_context(tc.tile_pool(name="reuse", bufs=1))
-        res = ctx.enter_context(tc.tile_pool(name="res", bufs=13))
+        res = ctx.enter_context(tc.tile_pool(name="res", bufs=15))
         psum_b = ctx.enter_context(tc.psum_pool(name="psum_b", bufs=1))
         psum = ctx.enter_context(tc.psum_pool(name="psum", bufs=6))
 
@@ -121,10 +121,8 @@ def tile_picked_neuron_lin_gelu_srt_p_kernel(tc, w_words, w_scales, xT, b, offs,
             plane = columns(bytes_a if t < SPLIT else bytes_b, t)
             y = res.tile([P, z - a], F32, name="y")
             acc = first_bank[:, P:] if (t, a) == (0, 0) else psum.tile([P, z - a], F32, name="acc")[:]
-            width = QUARTER if (t, a) == (0, HALF) else z - a
-            for c in range(a, z, width):
-                nc.tensor.matmul_mx(out=acc[:, c - a : c - a + width], lhsT=codes.bitcast(FP8X4), lhsT_scale=plane,
-                                    rhs=x_codes[:, c : c + width].bitcast(FP8X4), rhs_scale=x_scale[:, c : c + width], start=True, stop=True)
+            nc.tensor.matmul_mx(out=acc, lhsT=codes.bitcast(FP8X4), lhsT_scale=plane,
+                                rhs=x_codes[:, a:z].bitcast(FP8X4), rhs_scale=x_scale[:, a:z], start=True, stop=True)
             nc.scalar.activation(y[:], acc, GELU, bias=bias[t // 4][:, t % 4 : t % 4 + 1])
             nc.sync.dma_start(out[picked, a:z], y[:])
 
@@ -139,7 +137,9 @@ def tile_picked_neuron_lin_gelu_srt_p_kernel(tc, w_words, w_scales, xT, b, offs,
             cast(nc.vector.tensor_copy, 1, 1, a, a + QUARTER)
         for a in (0, QUARTER):
             quantize(1, a)
-        for t in range(SPLIT):
+        for a in (HALF, HALF + QUARTER):
+            product(0, a, a + QUARTER)
+        for t in range(1, SPLIT):
             product(t, HALF, T)
         gather(bytes_b, scale_table, EARLY, S)
         for t in range(SPLIT, TILES):

@@ -18,9 +18,9 @@ SPARE = N - S
 HALF = T // 2
 QUARTER = T // 4
 TILES = S // P
-SPLIT = 5
+SPLIT = 6
 EARLY = SPLIT * P
-WORD_CUTS = (0, 160, 384, EARLY)
+WORD_CUTS = (0, 192, 448, EARLY)
 
 
 def tile_picked_neuron_lin_gelu_srt_p_kernel(tc, w_words, w_scales, xT, b, offs, out):
@@ -28,7 +28,7 @@ def tile_picked_neuron_lin_gelu_srt_p_kernel(tc, w_words, w_scales, xT, b, offs,
     with ExitStack() as ctx:
         keep = ctx.enter_context(tc.tile_pool(name="keep", bufs=1))
         reuse = ctx.enter_context(tc.tile_pool(name="reuse", bufs=1))
-        res = ctx.enter_context(tc.tile_pool(name="res", bufs=15))
+        res = ctx.enter_context(tc.tile_pool(name="res", bufs=16))
         psum_b = ctx.enter_context(tc.psum_pool(name="psum_b", bufs=1))
         psum = ctx.enter_context(tc.psum_pool(name="psum", bufs=6))
 

@@ -20,7 +20,7 @@ QUARTER = T // 4
 TILES = S // P
 SPLIT = 6
 EARLY = SPLIT * P
-WORD_CUTS = (0, 192, 448, EARLY)
+WORD_CUTS = (0, 160, 384, EARLY)
 
 
 def tile_picked_neuron_lin_gelu_srt_p_kernel(tc, w_words, w_scales, xT, b, offs, out):
@@ -36,7 +36,7 @@ def tile_picked_neuron_lin_gelu_srt_p_kernel(tc, w_words, w_scales, xT, b, offs,
         nc.vector.memset(scale_table[:].bitcast(I32), 0)
         zero = keep.tile([P, 1], F32, name="zero")
         nc.vector.memset(zero[:], 0.0)
-        bias_rows = keep.tile([P, 2, P], F32, name="bias_rows", align_bytes=64)
+        bias_rows = keep.tile([P, P], F32, name="bias_rows", align_bytes=64)
         nc.vector.memset(bias_rows[:], 0.0)
 
         offsets = keep.tile([P, S // 16], U16, name="offsets")
@@ -59,7 +59,7 @@ def tile_picked_neuron_lin_gelu_srt_p_kernel(tc, w_words, w_scales, xT, b, offs,
         nc.scalar.activation(warm[:], zero[:], GELU)
         load_x(0, 1)
         load_words(0, WORD_CUTS[1] + SPARE)
-        nc.sync.dma_start(bias_rows[0 : TILES // 2, :, :], b.rearrange("(h c p) o -> c h (p o)", h=2, p=P))
+        nc.sync.dma_start(bias_rows[0:TILES, :], b.rearrange("(c p) o -> c (p o)", p=P))
         for a, z in zip(WORD_CUTS[1:], WORD_CUTS[2:]):
             load_words(a + SPARE, z + SPARE)
         load_x(1, 0)
@@ -101,11 +101,12 @@ def tile_picked_neuron_lin_gelu_srt_p_kernel(tc, w_words, w_scales, xT, b, offs,
             quantize(0, a)
 
         bias_ps = psum_b.tile([P, P], F32, name="bias_ps")
-        nc.tensor.transpose(bias_ps[:], bias_rows[:, 0, :], ident[:])
+        nc.tensor.transpose(bias_ps[:], bias_rows[:], ident[:])
         first_bank = psum_b.tile([P, P + HALF], F32, name="first_bank")
-        nc.tensor.transpose(first_bank[:, 0:P], bias_rows[:, 1, :], ident[:])
-        bias = [keep.tile([P, TILES // 2], F32, name="bias%d" % h) for h in range(2)]
-        nc.scalar.copy(bias[0][:], bias_ps[:, 0 : TILES // 2])
+        nc.tensor.transpose(first_bank[:, 0:P], bias_rows[:], ident[:])
+        bias_a = keep.tile([P, SPLIT], F32, name="bias_a")
+        nc.scalar.copy(bias_a[:], bias_ps[:, 0:SPLIT])
+        bias_b = reuse.tile([P, TILES - SPLIT], F32, name="bias_b", offset=2048 - 32)
 
         codes_a = (keep.tile([P, EARLY], U32, name="codes_a", align_bytes=64), 0)
         bytes_b = (reuse.tile([P, S - EARLY], U8, name="bytes_b", align_bytes=64, offset=0), EARLY)
@@ -123,15 +124,13 @@ def tile_picked_neuron_lin_gelu_srt_p_kernel(tc, w_words, w_scales, xT, b, offs,
             acc = first_bank[:, P:] if (t, a) == (0, 0) else psum.tile([P, z - a], F32, name="acc")[:]
             nc.tensor.matmul_mx(out=acc, lhsT=codes.bitcast(FP8X4), lhsT_scale=plane,
                                 rhs=x_codes[:, a:z].bitcast(FP8X4), rhs_scale=x_scale[:, a:z], start=True, stop=True)
-            nc.scalar.activation(y[:], acc, GELU, bias=bias[t // 4][:, t % 4 : t % 4 + 1])
+            nc.scalar.activation(y[:], acc, GELU, bias=bias_a[:, t : t + 1] if t < SPLIT else bias_b[:, t - SPLIT : t - SPLIT + 1])
             nc.sync.dma_start(out[picked, a:z], y[:])
 
         for a, z in zip(WORD_CUTS, WORD_CUTS[1:]):
             gather(codes_a, word_table, a, z)
         for t in range(SPLIT):
             product(t, 0, HALF)
-            if t == 0:
-                nc.scalar.copy(bias[1][:], first_bank[:, 0 : TILES // 2])
         cast(nc.vector.tensor_copy, 1, 0, 0, HALF)
         for a in (0, QUARTER):
             cast(nc.vector.tensor_copy, 1, 1, a, a + QUARTER)
@@ -142,6 +141,7 @@ def tile_picked_neuron_lin_gelu_srt_p_kernel(tc, w_words, w_scales, xT, b, offs,
         for t in range(1, SPLIT):
             product(t, HALF, T)
         gather(bytes_b, scale_table, EARLY, S)
+        nc.vector.tensor_copy(bias_b[:], first_bank[:, SPLIT:TILES])
         for t in range(SPLIT, TILES):
             gather(codes_b, word_table, t * P, (t + 1) * P, N)
             product(t, 0, T)

@@ -48,13 +48,16 @@ def tile_picked_neuron_lin_gelu_srt_p_kernel(tc, w_words, w_scales, xT, b, offs,
         def load_words(a, z):
             nc.sync.dma_start(word_table[:, a:z].bitcast(I32), w_flat[:, 4 * a : 4 * z].bitcast(I32))
 
+        def load_scales(a, z, queues):
+            for r in range(4):
+                queues[r % 2].dma_start(scale_table[r:P:32, a:z].bitcast(I32), w_scales[0, r:16:4, a:z].bitcast(I32))
+
         def load_x(u, e):
             nc.sync.dma_start(raw[u][e][:], x_rows[:, 2 * e : 2 * e + 2, u * HALF : (u + 1) * HALF])
 
         load_x(0, 0)
         nc.sync.dma_start(offsets[:], offs)
-        for r in range(4):
-            (nc.sync, nc.scalar)[r % 2].dma_start(scale_table[r:P:32, :].bitcast(I32), w_scales[0, r:16:4, :].bitcast(I32))
+        load_scales(0, EARLY + SPARE, (nc.sync, nc.scalar))
         warm = keep.tile([P, 1], F32, name="warm")
         nc.scalar.activation(warm[:], zero[:], GELU)
         load_x(0, 1)
@@ -64,7 +67,6 @@ def tile_picked_neuron_lin_gelu_srt_p_kernel(tc, w_words, w_scales, xT, b, offs,
             load_words(a + SPARE, z + SPARE)
         load_x(1, 0)
         load_x(1, 1)
-        load_words(EARLY + SPARE, N)
 
         ones = keep.tile([P, P], F32, name="ones")
         nc.vector.memset(ones[:], 1.0)
@@ -95,6 +97,8 @@ def tile_picked_neuron_lin_gelu_srt_p_kernel(tc, w_words, w_scales, xT, b, offs,
         bytes_a = (keep.tile([P, EARLY], U8, name="bytes_a", align_bytes=64), 0)
         cast(nc.scalar.copy, 0, 0, 0, HALF)
         gather(bytes_a, scale_table, 0, EARLY)
+        load_scales(EARLY + SPARE, N, (nc.sync, nc.sync))
+        load_words(EARLY + SPARE, N)
         for a in (0, QUARTER):
             cast(nc.scalar.copy, 0, 1, a, a + QUARTER)
         for a in (0, QUARTER):
@@ -116,15 +120,17 @@ def tile_picked_neuron_lin_gelu_srt_p_kernel(tc, w_words, w_scales, xT, b, offs,
             tile, first = piece
             return tile[:, t * P - first : (t + 1) * P - first]
 
-        def product(t, a, z):
+        def product(t, a, z, width=None):
             picked = slice(t * P, (t + 1) * P)
             codes = columns(codes_a if t < SPLIT else codes_b, t)
             plane = columns(bytes_a if t < SPLIT else bytes_b, t)
             y = res.tile([P, z - a], F32, name="y")
-            acc = first_bank[:, P:] if (t, a) == (0, 0) else psum.tile([P, z - a], F32, name="acc")[:]
-            nc.tensor.matmul_mx(out=acc, lhsT=codes.bitcast(FP8X4), lhsT_scale=plane,
-                                rhs=x_codes[:, a:z].bitcast(FP8X4), rhs_scale=x_scale[:, a:z], start=True, stop=True)
-            nc.scalar.activation(y[:], acc, GELU, bias=bias_a[:, t : t + 1] if t < SPLIT else bias_b[:, t - SPLIT : t - SPLIT + 1])
+            width = width or z - a
+            for c in range(a, z, width):
+                acc = first_bank[:, P:] if (t, c) == (0, 0) else psum.tile([P, width], F32, name="acc")[:]
+                nc.tensor.matmul_mx(out=acc, lhsT=codes.bitcast(FP8X4), lhsT_scale=plane,
+                                    rhs=x_codes[:, c : c + width].bitcast(FP8X4), rhs_scale=x_scale[:, c : c + width], start=True, stop=True)
+                nc.scalar.activation(y[:, c - a : c - a + width], acc, GELU, bias=bias_a[:, t : t + 1] if t < SPLIT else bias_b[:, t - SPLIT : t - SPLIT + 1])
             nc.sync.dma_start(out[picked, a:z], y[:])
 
         for a, z in zip(WORD_CUTS, WORD_CUTS[1:]):
@@ -136,8 +142,7 @@ def tile_picked_neuron_lin_gelu_srt_p_kernel(tc, w_words, w_scales, xT, b, offs,
             cast(nc.vector.tensor_copy, 1, 1, a, a + QUARTER)
         for a in (0, QUARTER):
             quantize(1, a)
-        for a in (HALF, HALF + QUARTER):
-            product(0, a, a + QUARTER)
+        product(0, HALF, T, QUARTER)
         for t in range(1, SPLIT):
             product(t, HALF, T)
         gather(bytes_b, scale_table, EARLY, S)

from contextlib import ExitStack

import concourse.mybir as mybir

K, T, S, N = 512, 512, 1024, 2048
FLOPS = 2 * K * T * S
F32 = mybir.dt.float32
BF16 = mybir.dt.bfloat16
I32 = mybir.dt.int32
U32 = mybir.dt.uint32
U16 = mybir.dt.uint16
U8 = mybir.dt.uint8
FP8X4 = mybir.dt.float8_e4m3fn_x4
ALU = mybir.AluOpType
GELU = mybir.ActivationFunctionType.Gelu_apprx_tanh
P = 128
SPARE = N - S
HALF = T // 2
QUARTER = T // 4
TILES = S // P
SPLIT = 6
EARLY = SPLIT * P
WORD_CUTS = (0, 160, 384, EARLY)


def tile_picked_neuron_lin_gelu_srt_p_kernel(tc, w_words, w_scales, xT, b, offs, out):
    nc = tc.nc
    with ExitStack() as ctx:
        keep = ctx.enter_context(tc.tile_pool(name="keep", bufs=1))
        reuse = ctx.enter_context(tc.tile_pool(name="reuse", bufs=1))
        res = ctx.enter_context(tc.tile_pool(name="res", bufs=16))
        psum_b = ctx.enter_context(tc.psum_pool(name="psum_b", bufs=1))
        psum = ctx.enter_context(tc.psum_pool(name="psum", bufs=6))

        scale_table = keep.tile([P, N], U8, name="scale_table", align_bytes=64)
        nc.vector.memset(scale_table[:].bitcast(I32), 0)
        zero = keep.tile([P, 1], F32, name="zero")
        nc.vector.memset(zero[:], 0.0)
        bias_rows = keep.tile([P, P], F32, name="bias_rows", align_bytes=64)
        nc.vector.memset(bias_rows[:], 0.0)

        offsets = keep.tile([P, S // 16], U16, name="offsets")
        x_rows = xT.rearrange("(p j) t -> p j t", j=4)
        raw = [[keep.tile([P, 2, HALF], F32, name="raw%d%d" % (u, e), align_bytes=64) for e in range(2)] for u in range(2)]
        word_table = keep.tile([P, N], U32, name="word_table", align_bytes=64)
        w_flat = w_words[0].rearrange("p n r -> p (n r)")

        def load_words(a, z):
            nc.sync.dma_start(word_table[:, a:z].bitcast(I32), w_flat[:, 4 * a : 4 * z].bitcast(I32))

        def load_scales(a, z, queues):
            for r in range(4):
                queues[r % 2].dma_start(scale_table[r:P:32, a:z].bitcast(I32), w_scales[0, r:16:4, a:z].bitcast(I32))

        def load_x(u, e):
            nc.sync.dma_start(raw[u][e][:], x_rows[:, 2 * e : 2 * e + 2, u * HALF : (u + 1) * HALF])

        load_x(0, 0)
        nc.sync.dma_start(offsets[:], offs)
        load_scales(0, EARLY + SPARE, (nc.sync, nc.scalar))
        warm = keep.tile([P, 1], F32, name="warm")
        nc.scalar.activation(warm[:], zero[:], GELU)
        load_x(0, 1)
        load_words(0, WORD_CUTS[1] + SPARE)
        nc.sync.dma_start(bias_rows[0:TILES, :], b.rearrange("(c p) o -> c (p o)", p=P))
        for a, z in zip(WORD_CUTS[1:], WORD_CUTS[2:]):
            load_words(a + SPARE, z + SPARE)
        load_x(1, 0)
        load_x(1, 1)

        ones = keep.tile([P, P], F32, name="ones")
        nc.vector.memset(ones[:], 1.0)
        column = keep.tile([P, P], F32, name="column", align_bytes=64)
        nc.vector.tensor_tensor_scan(column[:], ones[:], ones[:], -1.0, ALU.mult, ALU.add)
        turned = keep.tile([P, P], F32, name="turned", align_bytes=64)
        nc.vector.transpose(turned[:], column[:])
        ident = keep.tile([P, P], F32, name="ident")
        for q in range(0, P, 32):
            nc.vector.tensor_scalar(ident[q : q + 32, :], column[q : q + 32, :], turned[q : q + 32, q : q + 1], None, ALU.is_equal)

        def gather(dst, table, a, z, window=None):
            tile, first = dst
            nc.vector.tensor_copy(tile[:, a - first : z - first], table[:, 0 : window or z + SPARE].indirect(offsets[:, a // 16 : z // 16]))

        x_codes = keep.tile([P, T], U32, name="x_codes", align_bytes=64)
        x_scale = keep.tile([P, T], U8, name="x_scale", align_bytes=64)
        grouped = [keep.tile([P, HALF, 4], BF16, name="grouped0", align_bytes=64),
                   reuse.tile([P, HALF, 4], BF16, name="grouped1", align_bytes=64, offset=0)]

        def cast(copy, u, e, a, z):
            copy(grouped[u][:, a:z, 2 * e : 2 * e + 2], raw[u][e][:, :, a:z].rearrange("p j t -> p t j"))

        def quantize(u, a):
            cols = slice(u * HALF + a, u * HALF + a + QUARTER)
            nc.vector.quantize_mx(out=x_codes[:, cols].bitcast(FP8X4), scales=x_scale[:, cols], in_=grouped[u][:, a : a + QUARTER, :].rearrange("p t j -> p (t j)"))

        bytes_a = (keep.tile([P, EARLY], U8, name="bytes_a", align_bytes=64), 0)
        cast(nc.scalar.copy, 0, 0, 0, HALF)
        gather(bytes_a, scale_table, 0, EARLY)
        load_scales(EARLY + SPARE, N, (nc.sync, nc.sync))
        load_words(EARLY + SPARE, N)
        for a in (0, QUARTER):
            cast(nc.scalar.copy, 0, 1, a, a + QUARTER)
        for a in (0, QUARTER):
            quantize(0, a)

        bias_ps = psum_b.tile([P, P], F32, name="bias_ps")
        nc.tensor.transpose(bias_ps[:], bias_rows[:], ident[:])
        first_bank = psum_b.tile([P, P + HALF], F32, name="first_bank")
        nc.tensor.transpose(first_bank[:, 0:P], bias_rows[:], ident[:])
        bias_a = keep.tile([P, SPLIT], F32, name="bias_a")
        nc.scalar.copy(bias_a[:], bias_ps[:, 0:SPLIT])
        bias_b = reuse.tile([P, TILES - SPLIT], F32, name="bias_b", offset=2048 - 32)

        codes_a = (keep.tile([P, EARLY], U32, name="codes_a", align_bytes=64), 0)
        bytes_b = (reuse.tile([P, S - EARLY], U8, name="bytes_b", align_bytes=64, offset=0), EARLY)
        codes_b = (reuse.tile([P, S - EARLY], U32, name="codes_b", align_bytes=64, offset=S - EARLY), EARLY)

        def columns(piece, t):
            tile, first = piece
            return tile[:, t * P - first : (t + 1) * P - first]

        def product(t, a, z, width=None):
            picked = slice(t * P, (t + 1) * P)
            codes = columns(codes_a if t < SPLIT else codes_b, t)
            plane = columns(bytes_a if t < SPLIT else bytes_b, t)
            y = res.tile([P, z - a], F32, name="y")
            width = width or z - a
            for c in range(a, z, width):
                acc = first_bank[:, P:] if (t, c) == (0, 0) else psum.tile([P, width], F32, name="acc")[:]
                nc.tensor.matmul_mx(out=acc, lhsT=codes.bitcast(FP8X4), lhsT_scale=plane,
                                    rhs=x_codes[:, c : c + width].bitcast(FP8X4), rhs_scale=x_scale[:, c : c + width], start=True, stop=True)
                nc.scalar.activation(y[:, c - a : c - a + width], acc, GELU, bias=bias_a[:, t : t + 1] if t < SPLIT else bias_b[:, t - SPLIT : t - SPLIT + 1])
            nc.sync.dma_start(out[picked, a:z], y[:])

        for a, z in zip(WORD_CUTS, WORD_CUTS[1:]):
            gather(codes_a, word_table, a, z)
        for t in range(SPLIT):
            product(t, 0, HALF)
        cast(nc.vector.tensor_copy, 1, 0, 0, HALF)
        for a in (0, QUARTER):
            cast(nc.vector.tensor_copy, 1, 1, a, a + QUARTER)
        for a in (0, QUARTER):
            quantize(1, a)
        product(0, HALF, T, QUARTER)
        for t in range(1, SPLIT):
            product(t, HALF, T)
        gather(bytes_b, scale_table, EARLY, S)
        nc.vector.tensor_copy(bias_b[:], first_bank[:, SPLIT:TILES])
        for t in range(SPLIT, TILES):
            gather(codes_b, word_table, t * P, (t + 1) * P, N)
            product(t, 0, T)
